import numpy as np
import ml_dtypes


def mxq(x, axis, fmt="e4m3"):
    dtype, down = {"e4m3": (ml_dtypes.float8_e4m3fn, 7), "e5m2": (ml_dtypes.float8_e5m2, 14)}[fmt]
    v = np.moveaxis(np.asarray(x, np.float32).astype(ml_dtypes.bfloat16).astype(np.float64), axis, -1)
    blocks = v.reshape(v.shape[:-1] + (-1, 32))
    amax = np.abs(blocks).max(-1, keepdims=True)
    byte = np.maximum(np.where(amax > 0, np.frexp(amax)[1] - 1 + 127, 0) - down, 1)
    scale = np.exp2(byte - 127.0)
    codes = (blocks / scale).astype(np.float32).astype(dtype).astype(np.float64)
    return np.moveaxis((codes * scale).reshape(v.shape), -1, axis)


WIDE = False


def mx_kscale(k):
    if not WIDE:
        return np.ones(k)
    levels = np.array([18, -18])
    if k % 512:
        return np.exp2(np.random.permutation(np.resize(levels, k // 32))).repeat(32)
    a = np.empty((k // 512, 16))
    for p in range(k // 512):
        a[p, :8] = np.random.permutation(np.resize(levels, 8))
        for g in range(8):
            far = levels[np.abs(levels - a[p, g]) >= 10]
            a[p, g + 8] = far[np.random.randint(len(far))]
    return np.exp2(a.ravel()).repeat(32)


def f64(x):
    return np.asarray(x).astype(np.float64)


def striped(idx):
    return np.tile(np.asarray(idx).reshape(-1, 16).T, (8, 1)).astype(np.uint16)


def unstriped(offs):
    return offs[:16].T.reshape(-1).astype(np.int64)

def planes(y):
    n, m = y.shape
    v = y.astype(np.float32).astype(ml_dtypes.bfloat16).astype(np.float64).reshape(n // 32, 32, m)
    top = np.abs(v).max(1)
    byte = np.clip(np.where(top > 0, np.frexp(top)[1] - 1 + 127 - 7, 1), 1, 254)
    codes = (v * np.exp2(127.0 - byte)[:, None, :]).reshape(n, m).astype(np.float32).astype(ml_dtypes.float8_e4m3fn).view(np.uint8)
    words = codes.reshape(n // 512, 128, 4, m).transpose(0, 1, 3, 2)
    return np.ascontiguousarray(words), np.ascontiguousarray(byte.astype(np.uint8).reshape(n // 512, 16, m))


B, N, T, D, R = 1, 512, 2048, 512, 512
LR = 0.1
BETA = 0.9


def setup_inputs():
    n = np.random.standard_normal
    idx = np.random.permutation(T)[:B * N]
    s = mx_kscale(D)[:, None]
    z = mx_kscale(R)[:, None]
    x = n((B, D, R))
    return {
        "xT": (x * s).astype(np.float32),
        "wT": (n((D, T)) * (1.00 / np.sqrt(D)) / s).astype(np.float32),
        "y": n((B, R, N)).astype(np.float32),
        "wt": (np.random.uniform(0.5, 1.5, (B, R, 1)) * 1.0 / np.sqrt(R) * z).astype(np.float32),
        "xm": (x.transpose(0, 2, 1) / z / s[:, 0]).astype(np.float32),
        "mT": (0.3 * n((D, T)) / s).astype(np.float32),
        "offs": striped(idx),
    }


def reference(xT, wT, y, wt, xm, mT, offs):
    idx = unstriped(offs)
    pick = lambda x: x[:, idx].reshape(x.shape[0], B, N).transpose(1, 0, 2)
    w = pick(f64(wT))
    a = mxq(f64(xT), 1, "e4m3").transpose(0, 2, 1) @ mxq(w, 1, "e4m3")
    g = f64(wt) * (a - f64(y))
    dw = mxq(f64(xm), 1, "e4m3").transpose(0, 2, 1) @ mxq(g, 1, "e5m2")
    nm = BETA * pick(f64(mT)) + dw
    nw = w - LR * (dw + BETA * nm)
    tables = []
    for old, new in ((wT, nw), (mT, nm),):
        table = f64(old)
        table[:, idx] = new.transpose(1, 0, 2).reshape(D, B * N)
        tables.append(table)
    return tuple(tables) + planes(tables[0])

@@ -1,0 +1,175 @@
+from contextlib import ExitStack
+
+import concourse.mybir as mybir
+
+N, T, D, R = 512, 2048, 512, 512
+LR, BETA = 0.1, 0.9
+FLOPS = 4 * R * D * N
+
+F32 = mybir.dt.float32
+BF16 = mybir.dt.bfloat16
+I32 = mybir.dt.int32
+U32 = mybir.dt.uint32
+U16 = mybir.dt.uint16
+U8 = mybir.dt.uint8
+E4M3 = mybir.dt.float8_e4m3fn_x4
+E5M2 = mybir.dt.float8_e5m2_x4
+MULT = mybir.AluOpType.mult
+ADD = mybir.AluOpType.add
+SUB = mybir.AluOpType.subtract
+COPY = mybir.ActivationFunctionType.Copy
+
+P = 128
+L = 4
+CH = 512
+
+
+def tile_attend_gsq_pl_nag_kernel(tc, xT, wT, y, wt, xm, mT, offs, out_0, out_1, out_2, out_3):
+    nc = tc.nc
+    w_planes = wT.rearrange("(p j) t -> p j t", j=L)
+    m_planes = mT.rearrange("(p j) t -> p j t", j=L)
+    o0_planes = out_0.rearrange("(p j) t -> p j t", j=L)
+    o1_planes = out_1.rearrange("(p j) t -> p j t", j=L)
+    x_rows = xT[0].rearrange("(p j) r -> p j r", j=L)
+    xm_rows = xm[0].rearrange("(p j) d -> p j d", j=L)
+    y_rows = y[0].rearrange("(p j) n -> p j n", j=L)
+    words_out = out_2[0].rearrange("p t l -> p (t l)").bitcast(I32)
+    scales_out = out_3[0].bitcast(I32)
+
+    with ExitStack() as ctx:
+        keep = ctx.enter_context(tc.tile_pool(name="keep", bufs=1))
+        psum = ctx.enter_context(tc.psum_pool(name="psum", bufs=1))
+
+        def quantise(name, grouped, fmt, pieces):
+            width = grouped.shape[1] // L
+            codes = keep.tile([P, width], U32, name=name + "_codes", align_bytes=64)
+            scales = keep.tile([P, width], U8, name=name + "_scales", align_bytes=64)
+            step = width // pieces
+            for c in range(0, width, step):
+                nc.vector.quantize_mx(out=codes[:, c : c + step].bitcast(fmt), scales=scales[:, c : c + step], in_=grouped[:, L * c : L * (c + step)])
+            return codes, scales
+
+        def deal(dst, raw, half):
+            src = raw[:].rearrange("p t (s j) -> p s t j", j=L)
+            out = dst[:].rearrange("p (j s t) -> p s t j", j=L, t=L)[:, half * 64 : (half + 1) * 64]
+            nc.scalar.copy(out, src)
+
+        def weave(dst, src):
+            nc.vector.tensor_copy(dst[:].rearrange("p (c i t) -> p c t i", i=4, t=L), src[:].rearrange("p t (c i) -> p c t i", i=4))
+
+        offsets = keep.tile([P, N // 16], U16, name="offsets")
+        w_src = [keep.tile([P, T], F32, name=f"w_src{j}", tag=f"table{j}") for j in range(L)]
+        nc.sync.dma_start(w_src[0][:], w_planes[:, 0, :])
+        nc.sync.dma_start(offsets[:], offs)
+        for j in range(1, L):
+            nc.sync.dma_start(w_src[j][:], w_planes[:, j, :])
+        x_raw = [keep.tile([P, L, R // 2], F32, name=f"x_raw{h}") for h in range(2)]
+        for h in range(2):
+            nc.sync.dma_start(x_raw[h][:], x_rows[:, :, h * 256 : (h + 1) * 256])
+        weight = keep.tile([P, L], F32, name="weight")
+        nc.sync.dma_start(weight[:], wt[0].rearrange("(p j) o -> p (j o)", j=L))
+        target = [keep.tile([P, N], F32, name=f"target{j}") for j in range(L)]
+        for j in range(L):
+            nc.sync.dma_start(target[j][:], y_rows[:, j, :])
+        xm_raw = [keep.tile([P, L, D // 2], F32, name=f"xm_raw{h}", tag=("xm_raw0" if h == 0 else "late")) for h in range(2)]
+        for h in range(2):
+            nc.sync.dma_start(xm_raw[h][:], xm_rows[:, :, h * 256 : (h + 1) * 256])
+        m_src = [keep.tile([P, T], F32, name=f"m_src{j}") for j in range(L)]
+        for j in range(L):
+            nc.sync.dma_start(m_src[j][:], m_planes[:, j, :])
+
+        w_got = keep.tile([P, L, N], F32, name="w_got")
+        w_new = []
+        for j in range(L):
+            nc.vector.tensor_copy(w_got[:, j, :], w_src[j][:].indirect(offsets[:]))
+            if j < L - 1:
+                w_new.append(keep.tile([P, T], F32, name=f"w_new{j}"))
+                nc.scalar.activation(w_new[j][:], w_src[j][:], COPY)
+        w_bf = keep.tile([P, L * N], BF16, name="w_bf", align_bytes=64)
+        weave(w_bf, w_got)
+        w_codes, w_scales = quantise("w", w_bf, E4M3, 1)
+        x_bf = keep.tile([P, L * R], BF16, name="x_bf", align_bytes=64)
+        for h in range(2):
+            deal(x_bf, x_raw[h], h)
+        x_codes, x_scales = quantise("x", x_bf, E4M3, 4)
+
+        g_flat = keep.tile([P, L, N], BF16, name="g_flat")
+        for j in range(L):
+            cols = slice(j * P, (j + 1) * P)
+            score = psum.tile([P, N], F32, name=f"score{j}")
+            nc.tensor.matmul_mx(out=score[:], lhsT=x_codes[:, cols].bitcast(E4M3), lhsT_scale=x_scales[:, cols], rhs=w_codes[:].bitcast(E4M3), rhs_scale=w_scales[:], start=True, stop=True)
+            nc.scalar.activation(target[j][:], target[j][:], COPY, scale=weight[:, j : j + 1])
+            nc.vector.scalar_tensor_tensor(g_flat[:, j, :], score[:], weight[:, j : j + 1], target[j][:], MULT, SUB)
+        g_bf = keep.tile([P, L * N], BF16, name="g_bf", align_bytes=64)
+        weave(g_bf, g_flat)
+        xm_bf = keep.tile([P, L * D], BF16, name="xm_bf", tag="xm_bf", align_bytes=64)
+        for h in range(2):
+            deal(xm_bf, xm_raw[h], h)
+        g_codes, g_scales = quantise("g", g_bf, E5M2, 1)
+        xm_codes, xm_scales = quantise("xm", xm_bf, E4M3, 4)
+
+        dw = []
+        dw_step = []
+        for j in range(L):
+            cols = slice(j * P, (j + 1) * P)
+            grad = psum.tile([P, N], F32, name=f"grad{j}")
+            nc.tensor.matmul_mx(out=grad[:], lhsT=xm_codes[:, cols].bitcast(E4M3), lhsT_scale=xm_scales[:, cols], rhs=g_codes[:].bitcast(E5M2), rhs_scale=g_scales[:], start=True, stop=True)
+            dw_step.append(keep.tile([P, N], F32, name=f"dw_step{j}", tag=f"dw_step{j}"))
+            nc.scalar.activation(dw_step[j][:], grad[:], COPY, scale=-LR * (1.0 + BETA))
+            dw.append((keep.tile([P, N], F32, name=f"dw{j}"), grad))
+        for j in range(L):
+            nc.scalar.activation(dw[j][0][:], dw[j][1][:], COPY)
+        w_new.append(keep.tile([P, T], F32, name="w_new3", tag="late"))
+        nc.scalar.activation(w_new[L - 1][:], w_src[L - 1][:], COPY)
+
+        m_new = [keep.tile([P, T], F32, name=f"m_new{j}", tag=f"table{j}") for j in range(L)]
+        for j in range(L):
+            nc.sync.dma_start(m_new[j][:], m_planes[:, j, :])
+
+        chunks = T // CH
+        pairs = [keep.tile([P, 2, CH, 2], BF16, name=f"pairs{c}") for c in range(chunks)]
+        kept_first = keep.tile([P, N], F32, name="kept_first", tag="xm_bf", align_bytes=64)
+        kept = [kept_first[:]]
+
+        def gather_m(j):
+            nc.vector.tensor_scalar(kept[j], m_src[j][:].indirect(offsets[:]), BETA, 0.0, MULT, ADD)
+
+        def look_ahead(j):
+            nc.vector.scalar_tensor_tensor(w_got[:, j, :], kept[j], -LR * BETA, w_got[:, j, :], MULT, ADD)
+
+        def put_w(j):
+            nc.vector.tensor_tensor(w_new[j][:].indirect(offsets[:]), w_got[:, j, :], dw_step[j][:], ADD)
+            nc.sync.dma_start(o0_planes[:, j, :], w_new[j][:])
+            if j < L - 1:
+                for c in range(chunks):
+                    nc.scalar.copy(pairs[c][:, j // 2, :, j % 2], w_new[j][:, c * CH : (c + 1) * CH])
+
+        gather_m(0)
+        look_ahead(0)
+        put_w(0)
+        kept_rest = keep.tile([P, L - 1, N], F32, name="kept_rest", tag="dw_step0")
+        kept.extend([kept_rest[:, j, :] for j in range(L - 1)])
+        gather_m(1)
+        gather_m(2)
+        look_ahead(1)
+        gather_m(3)
+        look_ahead(2)
+        put_w(1)
+        look_ahead(3)
+        put_w(2)
+        put_w(3)
+
+        for j in range(L):
+            nc.vector.tensor_tensor(m_new[j][:].indirect(offsets[:]), kept[j], dw[j][0][:], ADD)
+            nc.sync.dma_start(o1_planes[:, j, :], m_new[j][:])
+        out_scales = keep.tile([P, T], U8, name="out_scales", align_bytes=64)
+        for c in range(chunks):
+            cols = slice(c * CH, (c + 1) * CH)
+            nc.scalar.copy(pairs[c][:, 1, :, 1], w_new[L - 1][:, cols])
+            out_bf = keep.tile([P, L * CH], BF16, name=f"out_bf{c}", align_bytes=64)
+            nc.scalar.copy(out_bf[:].bitcast(F32).rearrange("p (n u) -> p n u", u=2), pairs[c][:].rearrange("p u n e -> p u (n e)").bitcast(F32).rearrange("p u n -> p n u"))
+            out_codes = keep.tile([P, CH], U32, name=f"out_codes{c}", align_bytes=64)
+            nc.vector.quantize_mx(out=out_codes[:].bitcast(E4M3), scales=out_scales[:, cols], in_=out_bf[:])
+            nc.sync.dma_start(words_out[:, cols], out_codes[:].bitcast(I32))
+        for q in range(4):
+            nc.scalar.dma_start(scales_out[4 * q : 4 * q + 4, :], out_scales[32 * q : 32 * q + 4, :].bitcast(I32))

@@ -80,18 +80,19 @@ def tile_attend_gsq_pl_nag_kernel(tc, xT, wT, y, wt, xm, mT, offs, out_0, out_1,
 
         w_got = keep.tile([P, L, N], F32, name="w_got")
         w_new = []
+        w_bf = keep.tile([P, L * N], BF16, name="w_bf", align_bytes=64)
         for j in range(L):
             nc.vector.tensor_copy(w_got[:, j, :], w_src[j][:].indirect(offsets[:]))
+            if j % 2 == 1:
+                nc.vector.tensor_copy(w_bf[:].rearrange("p (n t) -> p n t", t=L)[:, :, j - 1 : j + 1], w_got[:, j - 1 : j + 1, :].rearrange("p t n -> p n t"))
             if j < L - 1:
                 w_new.append(keep.tile([P, T], F32, name=f"w_new{j}"))
                 nc.scalar.activation(w_new[j][:], w_src[j][:], COPY)
-        w_bf = keep.tile([P, L * N], BF16, name="w_bf", align_bytes=64)
-        weave(w_bf, w_got)
         w_codes, w_scales = quantise("w", w_bf, E4M3, 1)
         x_bf = keep.tile([P, L * R], BF16, name="x_bf", align_bytes=64)
         for h in range(2):
             deal(x_bf, x_raw[h], h)
-        x_codes, x_scales = quantise("x", x_bf, E4M3, 4)
+        x_codes, x_scales = quantise("x", x_bf, E4M3, 2)
 
         g_flat = keep.tile([P, L, N], BF16, name="g_flat")
         for j in range(L):
@@ -100,13 +101,13 @@ def tile_attend_gsq_pl_nag_kernel(tc, xT, wT, y, wt, xm, mT, offs, out_0, out_1,
             nc.tensor.matmul_mx(out=score[:], lhsT=x_codes[:, cols].bitcast(E4M3), lhsT_scale=x_scales[:, cols], rhs=w_codes[:].bitcast(E4M3), rhs_scale=w_scales[:], start=True, stop=True)
             nc.scalar.activation(target[j][:], target[j][:], COPY, scale=weight[:, j : j + 1])
             nc.vector.scalar_tensor_tensor(g_flat[:, j, :], score[:], weight[:, j : j + 1], target[j][:], MULT, SUB)
-        g_bf = keep.tile([P, L * N], BF16, name="g_bf", align_bytes=64)
+        g_bf = keep.tile([P, L * N], BF16, name="g_bf", tag="g_bf", align_bytes=64)
         weave(g_bf, g_flat)
         xm_bf = keep.tile([P, L * D], BF16, name="xm_bf", tag="xm_bf", align_bytes=64)
         for h in range(2):
             deal(xm_bf, xm_raw[h], h)
+        xm_codes, xm_scales = quantise("xm", xm_bf, E4M3, 1)
         g_codes, g_scales = quantise("g", g_bf, E5M2, 1)
-        xm_codes, xm_scales = quantise("xm", xm_bf, E4M3, 4)
 
         dw = []
         dw_step = []
@@ -116,7 +117,7 @@ def tile_attend_gsq_pl_nag_kernel(tc, xT, wT, y, wt, xm, mT, offs, out_0, out_1,
             nc.tensor.matmul_mx(out=grad[:], lhsT=xm_codes[:, cols].bitcast(E4M3), lhsT_scale=xm_scales[:, cols], rhs=g_codes[:].bitcast(E5M2), rhs_scale=g_scales[:], start=True, stop=True)
             dw_step.append(keep.tile([P, N], F32, name=f"dw_step{j}", tag=f"dw_step{j}"))
             nc.scalar.activation(dw_step[j][:], grad[:], COPY, scale=-LR * (1.0 + BETA))
-            dw.append((keep.tile([P, N], F32, name=f"dw{j}"), grad))
+            dw.append((keep.tile([P, N], F32, name=f"dw{j}", tag=f"dw{j}", align_bytes=64), grad))
         for j in range(L):
             nc.scalar.activation(dw[j][0][:], dw[j][1][:], COPY)
         w_new.append(keep.tile([P, T], F32, name="w_new3", tag="late"))
@@ -128,7 +129,7 @@ def tile_attend_gsq_pl_nag_kernel(tc, xT, wT, y, wt, xm, mT, offs, out_0, out_1,
 
         chunks = T // CH
         pairs = [keep.tile([P, 2, CH, 2], BF16, name=f"pairs{c}") for c in range(chunks)]
-        kept_first = keep.tile([P, N], F32, name="kept_first", tag="xm_bf", align_bytes=64)
+        kept_first = keep.tile([P, N], F32, name="kept_first", tag="g_bf", align_bytes=64)
         kept = [kept_first[:]]
 
         def gather_m(j):
@@ -149,27 +150,27 @@ def tile_attend_gsq_pl_nag_kernel(tc, xT, wT, y, wt, xm, mT, offs, out_0, out_1,
         put_w(0)
         kept_rest = keep.tile([P, L - 1, N], F32, name="kept_rest", tag="dw_step0")
         kept.extend([kept_rest[:, j, :] for j in range(L - 1)])
-        gather_m(1)
-        gather_m(2)
-        look_ahead(1)
-        gather_m(3)
-        look_ahead(2)
-        put_w(1)
-        look_ahead(3)
-        put_w(2)
-        put_w(3)
+        for j in range(1, L):
+            gather_m(j)
+        nc.vector.scalar_tensor_tensor(w_got[:, 1:, :], kept_rest[:], -LR * BETA, w_got[:, 1:, :], MULT, ADD)
+        for j in range(1, L):
+            put_w(j)
 
         for j in range(L):
             nc.vector.tensor_tensor(m_new[j][:].indirect(offsets[:]), kept[j], dw[j][0][:], ADD)
             nc.sync.dma_start(o1_planes[:, j, :], m_new[j][:])
-        out_scales = keep.tile([P, T], U8, name="out_scales", align_bytes=64)
+        out_scales = keep.tile([P, T], U8, name="out_scales", tag="dw3", align_bytes=64)
+        out_bf = [keep.tile([P, L * T // 2], BF16, name=f"out_bf{h}", align_bytes=64) for h in range(2)]
         for c in range(chunks):
             cols = slice(c * CH, (c + 1) * CH)
             nc.scalar.copy(pairs[c][:, 1, :, 1], w_new[L - 1][:, cols])
-            out_bf = keep.tile([P, L * CH], BF16, name=f"out_bf{c}", align_bytes=64)
-            nc.scalar.copy(out_bf[:].bitcast(F32).rearrange("p (n u) -> p n u", u=2), pairs[c][:].rearrange("p u n e -> p u (n e)").bitcast(F32).rearrange("p u n -> p n u"))
-            out_codes = keep.tile([P, CH], U32, name=f"out_codes{c}", align_bytes=64)
-            nc.vector.quantize_mx(out=out_codes[:].bitcast(E4M3), scales=out_scales[:, cols], in_=out_bf[:])
+            part = out_bf[c // 2][:, (c % 2) * L * CH : (c % 2 + 1) * L * CH]
+            nc.scalar.copy(part.bitcast(F32).rearrange("p (n u) -> p n u", u=2), pairs[c][:].rearrange("p u n e -> p u (n e)").bitcast(F32).rearrange("p u n -> p n u"))
+        for h in range(2):
+            cols = slice(h * T // 2, (h + 1) * T // 2)
+            out_codes = keep.tile([P, T // 2], U32, name=f"out_codes{h}", align_bytes=64)
+            nc.vector.quantize_mx(out=out_codes[:].bitcast(E4M3), scales=out_scales[:, cols], in_=out_bf[h][:])
+            if h == 1:
+                for q in range(4):
+                    nc.sync.dma_start(scales_out[4 * q : 4 * q + 4, :], out_scales[32 * q : 32 * q + 4, :].bitcast(I32))
             nc.sync.dma_start(words_out[:, cols], out_codes[:].bitcast(I32))
-        for q in range(4):
-            nc.scalar.dma_start(scales_out[4 * q : 4 * q + 4, :], out_scales[32 * q : 32 * q + 4, :].bitcast(I32))

@@ -1,6 +1,7 @@
 from contextlib import ExitStack
 
 import concourse.mybir as mybir
+from concourse.masks import make_identity
 
 N, T, D, R = 512, 2048, 512, 512
 LR, BETA = 0.1, 0.9
@@ -74,10 +75,12 @@ def tile_attend_gsq_pl_nag_kernel(tc, xT, wT, y, wt, xm, mT, offs, out_0, out_1,
         xm_raw = [keep.tile([P, L, D // 2], F32, name=f"xm_raw{h}", tag=("xm_raw0" if h == 0 else "late")) for h in range(2)]
         for h in range(2):
             nc.sync.dma_start(xm_raw[h][:], xm_rows[:, :, h * 256 : (h + 1) * 256])
-        m_src = [keep.tile([P, T], F32, name=f"m_src{j}") for j in range(L)]
+        m_src = [keep.tile([P, T], F32, name=f"m_src{j}", tag=f"m_src{j}") for j in range(L)]
         for j in range(L):
             nc.sync.dma_start(m_src[j][:], m_planes[:, j, :])
 
+        identity = keep.tile([P, P], F32, name="identity")
+        make_identity(nc, identity[:])
         w_got = keep.tile([P, L, N], F32, name="w_got")
         w_new = []
         w_bf = keep.tile([P, L * N], BF16, name="w_bf", align_bytes=64)
@@ -97,7 +100,7 @@ def tile_attend_gsq_pl_nag_kernel(tc, xT, wT, y, wt, xm, mT, offs, out_0, out_1,
         g_flat = keep.tile([P, L, N], BF16, name="g_flat")
         for j in range(L):
             cols = slice(j * P, (j + 1) * P)
-            score = psum.tile([P, N], F32, name=f"score{j}")
+            score = psum.tile([P, N], F32, name=f"score{j}", tag=f"score{j}")
             nc.tensor.matmul_mx(out=score[:], lhsT=x_codes[:, cols].bitcast(E4M3), lhsT_scale=x_scales[:, cols], rhs=w_codes[:].bitcast(E4M3), rhs_scale=w_scales[:], start=True, stop=True)
             nc.scalar.activation(target[j][:], target[j][:], COPY, scale=weight[:, j : j + 1])
             nc.vector.scalar_tensor_tensor(g_flat[:, j, :], score[:], weight[:, j : j + 1], target[j][:], MULT, SUB)
@@ -109,17 +112,11 @@ def tile_attend_gsq_pl_nag_kernel(tc, xT, wT, y, wt, xm, mT, offs, out_0, out_1,
         xm_codes, xm_scales = quantise("xm", xm_bf, E4M3, 1)
         g_codes, g_scales = quantise("g", g_bf, E5M2, 1)
 
-        dw = []
-        dw_step = []
+        grad = []
         for j in range(L):
             cols = slice(j * P, (j + 1) * P)
-            grad = psum.tile([P, N], F32, name=f"grad{j}")
-            nc.tensor.matmul_mx(out=grad[:], lhsT=xm_codes[:, cols].bitcast(E4M3), lhsT_scale=xm_scales[:, cols], rhs=g_codes[:].bitcast(E5M2), rhs_scale=g_scales[:], start=True, stop=True)
-            dw_step.append(keep.tile([P, N], F32, name=f"dw_step{j}", tag=f"dw_step{j}"))
-            nc.scalar.activation(dw_step[j][:], grad[:], COPY, scale=-LR * (1.0 + BETA))
-            dw.append((keep.tile([P, N], F32, name=f"dw{j}", tag=f"dw{j}", align_bytes=64), grad))
-        for j in range(L):
-            nc.scalar.activation(dw[j][0][:], dw[j][1][:], COPY)
+            grad.append(psum.tile([P, N], F32, name=f"grad{j}"))
+            nc.tensor.matmul_mx(out=grad[j][:], lhsT=xm_codes[:, cols].bitcast(E4M3), lhsT_scale=xm_scales[:, cols], rhs=g_codes[:].bitcast(E5M2), rhs_scale=g_scales[:], start=True, stop=True)
         w_new.append(keep.tile([P, T], F32, name="w_new3", tag="late"))
         nc.scalar.activation(w_new[L - 1][:], w_src[L - 1][:], COPY)
 
@@ -127,50 +124,82 @@ def tile_attend_gsq_pl_nag_kernel(tc, xT, wT, y, wt, xm, mT, offs, out_0, out_1,
         for j in range(L):
             nc.sync.dma_start(m_new[j][:], m_planes[:, j, :])
 
-        chunks = T // CH
-        pairs = [keep.tile([P, 2, CH, 2], BF16, name=f"pairs{c}") for c in range(chunks)]
-        kept_first = keep.tile([P, N], F32, name="kept_first", tag="g_bf", align_bytes=64)
-        kept = [kept_first[:]]
+        m_first = keep.tile([P, N], F32, name="m_first", tag="g_bf", align_bytes=64)
+        m_step = [m_first[:]]
+        kept = keep.tile([P, L, N], F32, name="kept")
 
         def gather_m(j):
-            nc.vector.tensor_scalar(kept[j], m_src[j][:].indirect(offsets[:]), BETA, 0.0, MULT, ADD)
-
-        def look_ahead(j):
-            nc.vector.scalar_tensor_tensor(w_got[:, j, :], kept[j], -LR * BETA, w_got[:, j, :], MULT, ADD)
+            nc.vector.tensor_scalar(m_step[j], m_src[j][:].indirect(offsets[:]), -LR * BETA * BETA, 0.0, MULT, ADD)
 
         def put_w(j):
-            nc.vector.tensor_tensor(w_new[j][:].indirect(offsets[:]), w_got[:, j, :], dw_step[j][:], ADD)
+            nc.vector.tensor_tensor(w_new[j][:].indirect(offsets[:]), descended[j], m_step[j], ADD)
             nc.sync.dma_start(o0_planes[:, j, :], w_new[j][:])
-            if j < L - 1:
-                for c in range(chunks):
-                    nc.scalar.copy(pairs[c][:, j // 2, :, j % 2], w_new[j][:, c * CH : (c + 1) * CH])
+
+        def round_plane(j):
+            nc.scalar.copy(pairs[:, j // 2, :, j % 2], w_new[j][:])
+
+        def put_m(j):
+            nc.vector.tensor_tensor(m_new[j][:].indirect(offsets[:]), kept[:, j, :], dw[j], ADD)
+            nc.sync.dma_start(o1_planes[:, j, :], m_new[j][:])
 
         gather_m(0)
-        look_ahead(0)
+        first = keep.tile([P, N], F32, name="first", tag="m_src0")
+        descended = [first[:]]
+        nc.vector.scalar_tensor_tensor(first[:], grad[0][:], -LR * (1.0 + BETA), w_got[:, 0, :], MULT, ADD)
         put_w(0)
-        kept_rest = keep.tile([P, L - 1, N], F32, name="kept_rest", tag="dw_step0")
-        kept.extend([kept_rest[:, j, :] for j in range(L - 1)])
+
+        dw_step = keep.tile([P, L - 1, N], F32, name="dw_step")
+        turned = keep.tile([P, L - 1, N], F32, name="turned", tag="pairs")
+        for j in range(1, L):
+            nc.scalar.activation(dw_step[:, j - 1, :], grad[j][:], COPY, scale=-LR * (1.0 + BETA))
+        for j in range(1, L):
+            there = psum.tile([P, N], F32, name=f"there{j}", tag=f"score{j}")
+            for c in range(N // P):
+                cols = slice(c * P, (c + 1) * P)
+                nc.tensor.matmul(there[:, cols], w_got[:, j, cols], identity[:], start=True, stop=False, is_transpose=True)
+                nc.tensor.matmul(there[:, cols], dw_step[:, j - 1, cols], identity[:], start=False, stop=True, is_transpose=True)
+            nc.scalar.copy(turned[:, j - 1, :], there[:])
+        dw_early = keep.tile([P, L - 1, N], F32, name="dw_early", tag="dw_early", align_bytes=64)
+        dw = [dw_early[:, j, :] for j in range(L - 1)]
+        for j in range(L - 1):
+            nc.scalar.activation(dw[j], grad[j][:], COPY)
+        nc.scalar.activation(kept[:, 0, :], m_first[:], COPY, scale=-1.0 / (LR * BETA))
+        for j in range(1, L):
+            back = psum.tile([P, N], F32, name=f"back{j}", tag=f"score{j}")
+            for c in range(N // P):
+                cols = slice(c * P, (c + 1) * P)
+                nc.tensor.transpose(back[:, cols], turned[:, j - 1, cols], identity[:])
+            nc.scalar.copy(w_got[:, j, :], back[:])
+            descended.append(w_got[:, j, :])
+
+        m_rest = keep.tile([P, L - 1, N], F32, name="m_rest", tag="m_src0")
+        m_step.extend([m_rest[:, j, :] for j in range(L - 1)])
         for j in range(1, L):
             gather_m(j)
-        nc.vector.scalar_tensor_tensor(w_got[:, 1:, :], kept_rest[:], -LR * BETA, w_got[:, 1:, :], MULT, ADD)
         for j in range(1, L):
             put_w(j)
+        pairs = keep.tile([P, 2, T, 2], BF16, name="pairs", tag="pairs")
+        round_plane(0)
+        round_plane(1)
+        round_plane(2)
+        nc.scalar.activation(kept[:, 1:, :], m_rest[:], COPY, scale=-1.0 / (LR * BETA))
+        round_plane(3)
 
-        for j in range(L):
-            nc.vector.tensor_tensor(m_new[j][:].indirect(offsets[:]), kept[j], dw[j][0][:], ADD)
-            nc.sync.dma_start(o1_planes[:, j, :], m_new[j][:])
-        out_scales = keep.tile([P, T], U8, name="out_scales", tag="dw3", align_bytes=64)
-        out_bf = [keep.tile([P, L * T // 2], BF16, name=f"out_bf{h}", align_bytes=64) for h in range(2)]
-        for c in range(chunks):
-            cols = slice(c * CH, (c + 1) * CH)
-            nc.scalar.copy(pairs[c][:, 1, :, 1], w_new[L - 1][:, cols])
-            part = out_bf[c // 2][:, (c % 2) * L * CH : (c % 2 + 1) * L * CH]
-            nc.scalar.copy(part.bitcast(F32).rearrange("p (n u) -> p n u", u=2), pairs[c][:].rearrange("p u n e -> p u (n e)").bitcast(F32).rearrange("p u n -> p n u"))
+        for j in range(L - 1):
+            put_m(j)
+        out_scales = keep.tile([P, T], U8, name="out_scales", tag="dw_early", align_bytes=64)
+        out_bf = [keep.tile([P, L * T // 2], BF16, name=f"out_bf{h}", tag=f"out_bf{h}", align_bytes=64) for h in range(2)]
+        pair_words = pairs[:].rearrange("p u n e -> p u (n e)").bitcast(F32)
+        for h in range(2):
+            nc.scalar.copy(out_bf[h][:].bitcast(F32).rearrange("p (n u) -> p n u", u=2), pair_words[:, :, h * T // 2 : (h + 1) * T // 2].rearrange("p u n -> p n u"))
         for h in range(2):
             cols = slice(h * T // 2, (h + 1) * T // 2)
             out_codes = keep.tile([P, T // 2], U32, name=f"out_codes{h}", align_bytes=64)
             nc.vector.quantize_mx(out=out_codes[:].bitcast(E4M3), scales=out_scales[:, cols], in_=out_bf[h][:])
-            if h == 1:
-                for q in range(4):
-                    nc.sync.dma_start(scales_out[4 * q : 4 * q + 4, :], out_scales[32 * q : 32 * q + 4, :].bitcast(I32))
             nc.sync.dma_start(words_out[:, cols], out_codes[:].bitcast(I32))
+        for q in range(4):
+            nc.sync.dma_start(scales_out[4 * q : 4 * q + 4, :], out_scales[32 * q : 32 * q + 4, :].bitcast(I32))
+        dw_last = keep.tile([P, N], F32, name="dw_last", tag="out_bf0", align_bytes=64)
+        dw.append(dw_last[:])
+        nc.scalar.activation(dw[L - 1], grad[L - 1][:], COPY)
+        put_m(L - 1)

@@ -41,22 +41,23 @@ def tile_attend_gsq_pl_nag_kernel(tc, xT, wT, y, wt, xm, mT, offs, out_0, out_1,
         keep = ctx.enter_context(tc.tile_pool(name="keep", bufs=1))
         psum = ctx.enter_context(tc.psum_pool(name="psum", bufs=1))
 
-        def quantise(name, grouped, fmt, pieces):
+        def quantise(name, grouped, fmt, widths):
             width = grouped.shape[1] // L
             codes = keep.tile([P, width], U32, name=name + "_codes", align_bytes=64)
             scales = keep.tile([P, width], U8, name=name + "_scales", align_bytes=64)
-            step = width // pieces
-            for c in range(0, width, step):
+            c = 0
+            for step in widths:
                 nc.vector.quantize_mx(out=codes[:, c : c + step].bitcast(fmt), scales=scales[:, c : c + step], in_=grouped[:, L * c : L * (c + step)])
+                c = c + step
             return codes, scales
 
-        def deal(dst, raw, half):
-            src = raw[:].rearrange("p t (s j) -> p s t j", j=L)
-            out = dst[:].rearrange("p (j s t) -> p s t j", j=L, t=L)[:, half * 64 : (half + 1) * 64]
+        def deal(dst, raw, half, tiles=slice(0, L)):
+            src = raw[:].rearrange("p t (s j) -> p s t j", j=L)[:, :, :, tiles]
+            out = dst[:].rearrange("p (j s t) -> p s t j", j=L, t=L)[:, half * 64 : (half + 1) * 64, :, tiles]
             nc.scalar.copy(out, src)
 
         def weave(dst, src):
-            nc.vector.tensor_copy(dst[:].rearrange("p (c i t) -> p c t i", i=4, t=L), src[:].rearrange("p t (c i) -> p c t i", i=4))
+            nc.vector.tensor_copy(dst.rearrange("p (c i t) -> p c t i", i=4, t=L), src.rearrange("p t (c i) -> p c t i", i=4))
 
         offsets = keep.tile([P, N // 16], U16, name="offsets")
         w_src = [keep.tile([P, T], F32, name=f"w_src{j}", tag=f"table{j}") for j in range(L)]
@@ -79,43 +80,56 @@ def tile_attend_gsq_pl_nag_kernel(tc, xT, wT, y, wt, xm, mT, offs, out_0, out_1,
         for j in range(L):
             nc.sync.dma_start(m_src[j][:], m_planes[:, j, :])
 
-        identity = keep.tile([P, P], F32, name="identity")
+        identity = keep.tile([P, P], F32, name="identity", tag="terms")
         make_identity(nc, identity[:])
         w_got = keep.tile([P, L, N], F32, name="w_got")
         w_new = []
         w_bf = keep.tile([P, L * N], BF16, name="w_bf", align_bytes=64)
+        halves = [slice(0, N // 2), slice(N // 2, N)]
         for j in range(L):
-            nc.vector.tensor_copy(w_got[:, j, :], w_src[j][:].indirect(offsets[:]))
+            parts = halves if j == L - 1 else [slice(0, N)]
+            for part in parts:
+                nc.vector.tensor_copy(w_got[:, j, part], w_src[j][:].indirect(offsets[:, part.start // 16 : part.stop // 16]))
             if j % 2 == 1:
-                nc.vector.tensor_copy(w_bf[:].rearrange("p (n t) -> p n t", t=L)[:, :, j - 1 : j + 1], w_got[:, j - 1 : j + 1, :].rearrange("p t n -> p n t"))
+                for part in parts:
+                    nc.vector.tensor_copy(w_bf[:].rearrange("p (n t) -> p n t", t=L)[:, part, j - 1 : j + 1], w_got[:, j - 1 : j + 1, part].rearrange("p t n -> p n t"))
             if j < L - 1:
                 w_new.append(keep.tile([P, T], F32, name=f"w_new{j}"))
                 nc.scalar.activation(w_new[j][:], w_src[j][:], COPY)
-        w_codes, w_scales = quantise("w", w_bf, E4M3, 1)
+        w_codes, w_scales = quantise("w", w_bf, E4M3, (256, 256))
         x_bf = keep.tile([P, L * R], BF16, name="x_bf", align_bytes=64)
-        for h in range(2):
-            deal(x_bf, x_raw[h], h)
-        x_codes, x_scales = quantise("x", x_bf, E4M3, 2)
+        deal(x_bf, x_raw[0], 0)
+        deal(x_bf, x_raw[1], 1, slice(0, 2))
+        deal(x_bf, x_raw[1], 1, slice(2, 4))
+        x_codes, x_scales = quantise("x", x_bf, E4M3, (128, 128, 256))
 
         g_flat = keep.tile([P, L, N], BF16, name="g_flat")
         for j in range(L):
             cols = slice(j * P, (j + 1) * P)
-            score = psum.tile([P, N], F32, name=f"score{j}", tag=f"score{j}")
-            nc.tensor.matmul_mx(out=score[:], lhsT=x_codes[:, cols].bitcast(E4M3), lhsT_scale=x_scales[:, cols], rhs=w_codes[:].bitcast(E4M3), rhs_scale=w_scales[:], start=True, stop=True)
             nc.scalar.activation(target[j][:], target[j][:], COPY, scale=weight[:, j : j + 1])
-            nc.vector.scalar_tensor_tensor(g_flat[:, j, :], score[:], weight[:, j : j + 1], target[j][:], MULT, SUB)
+            if j == 0:
+                for h, part in enumerate(halves):
+                    score = psum.tile([P, N], F32, name=f"score0_{h}", tag=("score0", "grad3")[h])
+                    nc.tensor.matmul_mx(out=score[:, part], lhsT=x_codes[:, cols].bitcast(E4M3), lhsT_scale=x_scales[:, cols], rhs=w_codes[:, part].bitcast(E4M3), rhs_scale=w_scales[:, part], start=True, stop=True)
+                    nc.vector.scalar_tensor_tensor(g_flat[:, j, part], score[:, part], weight[:, j : j + 1], target[j][:, part], MULT, SUB)
+            else:
+                score = psum.tile([P, N], F32, name=f"score{j}", tag=f"score{j}")
+                nc.tensor.matmul_mx(out=score[:], lhsT=x_codes[:, cols].bitcast(E4M3), lhsT_scale=x_scales[:, cols], rhs=w_codes[:].bitcast(E4M3), rhs_scale=w_scales[:], start=True, stop=True)
+                for part in halves if j == L - 1 else [slice(0, N)]:
+                    nc.vector.scalar_tensor_tensor(g_flat[:, j, part], score[:, part], weight[:, j : j + 1], target[j][:, part], MULT, SUB)
         g_bf = keep.tile([P, L * N], BF16, name="g_bf", tag="g_bf", align_bytes=64)
-        weave(g_bf, g_flat)
+        for part in halves:
+            weave(g_bf[:, L * part.start : L * part.stop], g_flat[:, :, part])
         xm_bf = keep.tile([P, L * D], BF16, name="xm_bf", tag="xm_bf", align_bytes=64)
         for h in range(2):
             deal(xm_bf, xm_raw[h], h)
-        xm_codes, xm_scales = quantise("xm", xm_bf, E4M3, 1)
-        g_codes, g_scales = quantise("g", g_bf, E5M2, 1)
+        g_codes, g_scales = quantise("g", g_bf, E5M2, (256, 256))
+        xm_codes, xm_scales = quantise("xm", xm_bf, E4M3, (512,))
 
         grad = []
         for j in range(L):
             cols = slice(j * P, (j + 1) * P)
-            grad.append(psum.tile([P, N], F32, name=f"grad{j}"))
+            grad.append(psum.tile([P, N], F32, name=f"grad{j}", tag=f"grad{j}"))
             nc.tensor.matmul_mx(out=grad[j][:], lhsT=xm_codes[:, cols].bitcast(E4M3), lhsT_scale=xm_scales[:, cols], rhs=g_codes[:].bitcast(E5M2), rhs_scale=g_scales[:], start=True, stop=True)
         w_new.append(keep.tile([P, T], F32, name="w_new3", tag="late"))
         nc.scalar.activation(w_new[L - 1][:], w_src[L - 1][:], COPY)
@@ -125,8 +139,8 @@ def tile_attend_gsq_pl_nag_kernel(tc, xT, wT, y, wt, xm, mT, offs, out_0, out_1,
             nc.sync.dma_start(m_new[j][:], m_planes[:, j, :])
 
         m_first = keep.tile([P, N], F32, name="m_first", tag="g_bf", align_bytes=64)
-        m_step = [m_first[:]]
-        kept = keep.tile([P, L, N], F32, name="kept")
+        m_rest = keep.tile([P, L - 1, N], F32, name="m_rest")
+        m_step = [m_first[:]] + [m_rest[:, j, :] for j in range(L - 1)]
 
         def gather_m(j):
             nc.vector.tensor_scalar(m_step[j], m_src[j][:].indirect(offsets[:]), -LR * BETA * BETA, 0.0, MULT, ADD)
@@ -138,17 +152,21 @@ def tile_attend_gsq_pl_nag_kernel(tc, xT, wT, y, wt, xm, mT, offs, out_0, out_1,
         def round_plane(j):
             nc.scalar.copy(pairs[:, j // 2, :, j % 2], w_new[j][:])
 
+        def momentum_terms(j):
+            nc.scalar.activation(dw[:, j, :], grad[j][:], COPY)
+            nc.scalar.activation(kept[j], m_step[j], COPY, scale=-1.0 / (LR * BETA))
+
         def put_m(j):
-            nc.vector.tensor_tensor(m_new[j][:].indirect(offsets[:]), kept[:, j, :], dw[j], ADD)
+            nc.vector.tensor_tensor(m_new[j][:].indirect(offsets[:]), kept[j], dw[:, j, :], ADD)
             nc.sync.dma_start(o1_planes[:, j, :], m_new[j][:])
 
         gather_m(0)
         first = keep.tile([P, N], F32, name="first", tag="m_src0")
-        descended = [first[:]]
+        descended = [first[:]] + [w_got[:, j, :] for j in range(1, L)]
         nc.vector.scalar_tensor_tensor(first[:], grad[0][:], -LR * (1.0 + BETA), w_got[:, 0, :], MULT, ADD)
         put_w(0)
 
-        dw_step = keep.tile([P, L - 1, N], F32, name="dw_step")
+        dw_step = keep.tile([P, L - 1, N], F32, name="dw_step", tag="dw_step")
         turned = keep.tile([P, L - 1, N], F32, name="turned", tag="pairs")
         for j in range(1, L):
             nc.scalar.activation(dw_step[:, j - 1, :], grad[j][:], COPY, scale=-LR * (1.0 + BETA))
@@ -159,36 +177,33 @@ def tile_attend_gsq_pl_nag_kernel(tc, xT, wT, y, wt, xm, mT, offs, out_0, out_1,
                 nc.tensor.matmul(there[:, cols], w_got[:, j, cols], identity[:], start=True, stop=False, is_transpose=True)
                 nc.tensor.matmul(there[:, cols], dw_step[:, j - 1, cols], identity[:], start=False, stop=True, is_transpose=True)
             nc.scalar.copy(turned[:, j - 1, :], there[:])
-        dw_early = keep.tile([P, L - 1, N], F32, name="dw_early", tag="dw_early", align_bytes=64)
-        dw = [dw_early[:, j, :] for j in range(L - 1)]
-        for j in range(L - 1):
-            nc.scalar.activation(dw[j], grad[j][:], COPY)
-        nc.scalar.activation(kept[:, 0, :], m_first[:], COPY, scale=-1.0 / (LR * BETA))
+        back = {}
         for j in range(1, L):
-            back = psum.tile([P, N], F32, name=f"back{j}", tag=f"score{j}")
+            back[j] = psum.tile([P, N], F32, name=f"back{j}", tag=f"score{j}")
             for c in range(N // P):
                 cols = slice(c * P, (c + 1) * P)
-                nc.tensor.transpose(back[:, cols], turned[:, j - 1, cols], identity[:])
-            nc.scalar.copy(w_got[:, j, :], back[:])
-            descended.append(w_got[:, j, :])
+                nc.tensor.transpose(back[j][:, cols], turned[:, j - 1, cols], identity[:])
+            nc.scalar.copy(descended[j], back[j][:])
+        pairs = keep.tile([P, 2, T, 2], BF16, name="pairs", tag="pairs")
+        round_plane(0)
+        terms = keep.tile([P, 2 * L - 1, N], F32, name="terms", tag="terms")
+        dw = terms[:, :L, :]
+        kept = [terms[:, L + j, :] for j in range(L - 1)]
+        momentum_terms(0)
 
-        m_rest = keep.tile([P, L - 1, N], F32, name="m_rest", tag="m_src0")
-        m_step.extend([m_rest[:, j, :] for j in range(L - 1)])
         for j in range(1, L):
             gather_m(j)
         for j in range(1, L):
             put_w(j)
-        pairs = keep.tile([P, 2, T, 2], BF16, name="pairs", tag="pairs")
-        round_plane(0)
-        round_plane(1)
-        round_plane(2)
-        nc.scalar.activation(kept[:, 1:, :], m_rest[:], COPY, scale=-1.0 / (LR * BETA))
-        round_plane(3)
+        for j in range(1, L - 1):
+            momentum_terms(j)
+            round_plane(j)
+        round_plane(L - 1)
 
         for j in range(L - 1):
             put_m(j)
-        out_scales = keep.tile([P, T], U8, name="out_scales", tag="dw_early", align_bytes=64)
-        out_bf = [keep.tile([P, L * T // 2], BF16, name=f"out_bf{h}", tag=f"out_bf{h}", align_bytes=64) for h in range(2)]
+        out_scales = keep.tile([P, T], U8, name="out_scales", align_bytes=64)
+        out_bf = [keep.tile([P, L * T // 2], BF16, name=f"out_bf{h}", align_bytes=64) for h in range(2)]
         pair_words = pairs[:].rearrange("p u n e -> p u (n e)").bitcast(F32)
         for h in range(2):
             nc.scalar.copy(out_bf[h][:].bitcast(F32).rearrange("p (n u) -> p n u", u=2), pair_words[:, :, h * T // 2 : (h + 1) * T // 2].rearrange("p u n -> p n u"))
@@ -199,7 +214,7 @@ def tile_attend_gsq_pl_nag_kernel(tc, xT, wT, y, wt, xm, mT, offs, out_0, out_1,
             nc.sync.dma_start(words_out[:, cols], out_codes[:].bitcast(I32))
         for q in range(4):
             nc.sync.dma_start(scales_out[4 * q : 4 * q + 4, :], out_scales[32 * q : 32 * q + 4, :].bitcast(I32))
-        dw_last = keep.tile([P, N], F32, name="dw_last", tag="out_bf0", align_bytes=64)
-        dw.append(dw_last[:])
-        nc.scalar.activation(dw[L - 1], grad[L - 1][:], COPY)
+        kept_last = keep.tile([P, N], F32, name="kept_last", tag="pairs")
+        kept.append(kept_last[:])
+        momentum_terms(L - 1)
         put_m(L - 1)

@@ -51,10 +51,10 @@ def tile_attend_gsq_pl_nag_kernel(tc, xT, wT, y, wt, xm, mT, offs, out_0, out_1,
                 c = c + step
             return codes, scales
 
-        def deal(dst, raw, half, tiles=slice(0, L)):
+        def deal(dst, raw, tiles, copy):
             src = raw[:].rearrange("p t (s j) -> p s t j", j=L)[:, :, :, tiles]
-            out = dst[:].rearrange("p (j s t) -> p s t j", j=L, t=L)[:, half * 64 : (half + 1) * 64, :, tiles]
-            nc.scalar.copy(out, src)
+            out = dst[:].rearrange("p (j s t) -> p s t j", j=L, t=L)[:, :, :, tiles]
+            copy(out, src)
 
         def weave(dst, src):
             nc.vector.tensor_copy(dst.rearrange("p (c i t) -> p c t i", i=4, t=L), src.rearrange("p t (c i) -> p c t i", i=4))
@@ -65,17 +65,16 @@ def tile_attend_gsq_pl_nag_kernel(tc, xT, wT, y, wt, xm, mT, offs, out_0, out_1,
         nc.sync.dma_start(offsets[:], offs)
         for j in range(1, L):
             nc.sync.dma_start(w_src[j][:], w_planes[:, j, :])
-        x_raw = [keep.tile([P, L, R // 2], F32, name=f"x_raw{h}") for h in range(2)]
-        for h in range(2):
-            nc.sync.dma_start(x_raw[h][:], x_rows[:, :, h * 256 : (h + 1) * 256])
+        x_raw = keep.tile([P, L, R], F32, name="x_raw")
+        nc.sync.dma_start(x_raw[:], x_rows)
         weight = keep.tile([P, L], F32, name="weight")
         nc.sync.dma_start(weight[:], wt[0].rearrange("(p j) o -> p (j o)", j=L))
-        target = [keep.tile([P, N], F32, name=f"target{j}") for j in range(L)]
-        for j in range(L):
-            nc.sync.dma_start(target[j][:], y_rows[:, j, :])
-        xm_raw = [keep.tile([P, L, D // 2], F32, name=f"xm_raw{h}", tag=("xm_raw0" if h == 0 else "late")) for h in range(2)]
-        for h in range(2):
-            nc.sync.dma_start(xm_raw[h][:], xm_rows[:, :, h * 256 : (h + 1) * 256])
+        target_pairs = [keep.tile([P, 2, N], F32, name=f"target{u}") for u in range(2)]
+        for u in range(2):
+            nc.sync.dma_start(target_pairs[u][:], y_rows[:, 2 * u : 2 * u + 2, :])
+        target = [target_pairs[j // 2][:, j % 2, :] for j in range(L)]
+        xm_raw = keep.tile([P, L, D], F32, name="xm_raw", tag="late")
+        nc.sync.dma_start(xm_raw[:], xm_rows)
         m_src = [keep.tile([P, T], F32, name=f"m_src{j}", tag=f"m_src{j}") for j in range(L)]
         for j in range(L):
             nc.sync.dma_start(m_src[j][:], m_planes[:, j, :])
@@ -98,15 +97,14 @@ def tile_attend_gsq_pl_nag_kernel(tc, xT, wT, y, wt, xm, mT, offs, out_0, out_1,
                 nc.scalar.activation(w_new[j][:], w_src[j][:], COPY)
         w_codes, w_scales = quantise("w", w_bf, E4M3, (256, 256))
         x_bf = keep.tile([P, L * R], BF16, name="x_bf", align_bytes=64)
-        deal(x_bf, x_raw[0], 0)
-        deal(x_bf, x_raw[1], 1, slice(0, 2))
-        deal(x_bf, x_raw[1], 1, slice(2, 4))
+        deal(x_bf, x_raw, slice(0, 2), nc.vector.tensor_copy)
+        deal(x_bf, x_raw, slice(2, 4), nc.scalar.copy)
         x_codes, x_scales = quantise("x", x_bf, E4M3, (128, 128, 256))
 
         g_flat = keep.tile([P, L, N], BF16, name="g_flat")
         for j in range(L):
             cols = slice(j * P, (j + 1) * P)
-            nc.scalar.activation(target[j][:], target[j][:], COPY, scale=weight[:, j : j + 1])
+            nc.scalar.activation(target[j], target[j], COPY, scale=weight[:, j : j + 1])
             if j == 0:
                 for h, part in enumerate(halves):
                     score = psum.tile([P, N], F32, name=f"score0_{h}", tag=("score0", "grad3")[h])
@@ -121,10 +119,10 @@ def tile_attend_gsq_pl_nag_kernel(tc, xT, wT, y, wt, xm, mT, offs, out_0, out_1,
         for part in halves:
             weave(g_bf[:, L * part.start : L * part.stop], g_flat[:, :, part])
         xm_bf = keep.tile([P, L * D], BF16, name="xm_bf", tag="xm_bf", align_bytes=64)
-        for h in range(2):
-            deal(xm_bf, xm_raw[h], h)
+        deal(xm_bf, xm_raw, slice(0, 2), nc.scalar.copy)
+        deal(xm_bf, xm_raw, slice(2, 4), nc.scalar.copy)
         g_codes, g_scales = quantise("g", g_bf, E5M2, (256, 256))
-        xm_codes, xm_scales = quantise("xm", xm_bf, E4M3, (512,))
+        xm_codes, xm_scales = quantise("xm", xm_bf, E4M3, (256, 256))
 
         grad = []
         for j in range(L):

@@ -104,7 +104,10 @@ def tile_attend_gsq_pl_nag_kernel(tc, xT, wT, y, wt, xm, mT, offs, out_0, out_1,
         g_flat = keep.tile([P, L, N], BF16, name="g_flat")
         for j in range(L):
             cols = slice(j * P, (j + 1) * P)
-            nc.scalar.activation(target[j], target[j], COPY, scale=weight[:, j : j + 1])
+            if j == 0:
+                nc.vector.tensor_scalar_mul(target[j], target[j], weight[:, j : j + 1])
+            else:
+                nc.scalar.activation(target[j], target[j], COPY, scale=weight[:, j : j + 1])
             if j == 0:
                 for h, part in enumerate(halves):
                     score = psum.tile([P, N], F32, name=f"score0_{h}", tag=("score0", "grad3")[h])

@@ -1,7 +1,6 @@
 from contextlib import ExitStack
 
 import concourse.mybir as mybir
-from concourse.masks import make_identity
 
 N, T, D, R = 512, 2048, 512, 512
 LR, BETA = 0.1, 0.9
@@ -22,7 +21,8 @@ COPY = mybir.ActivationFunctionType.Copy
 
 P = 128
 L = 4
-CH = 512
+GRAD_STEP = -LR * (1.0 + BETA)
+MOM_STEP = -LR * BETA * BETA
 
 
 def tile_attend_gsq_pl_nag_kernel(tc, xT, wT, y, wt, xm, mT, offs, out_0, out_1, out_2, out_3):
@@ -36,14 +36,19 @@ def tile_attend_gsq_pl_nag_kernel(tc, xT, wT, y, wt, xm, mT, offs, out_0, out_1,
     y_rows = y[0].rearrange("(p j) n -> p j n", j=L)
     words_out = out_2[0].rearrange("p t l -> p (t l)").bitcast(I32)
     scales_out = out_3[0].bitcast(I32)
+    halves = [slice(0, N // 2), slice(N // 2, N)]
+    whole = [slice(0, N)]
 
     with ExitStack() as ctx:
         keep = ctx.enter_context(tc.tile_pool(name="keep", bufs=1))
         psum = ctx.enter_context(tc.psum_pool(name="psum", bufs=1))
 
-        def quantise(name, grouped, fmt, widths):
+        def listed(window, part):
+            return window[:].indirect(offsets[:, part.start // 16 : part.stop // 16])
+
+        def quantise(name, grouped, fmt, widths, tag=None):
             width = grouped.shape[1] // L
-            codes = keep.tile([P, width], U32, name=name + "_codes", align_bytes=64)
+            codes = keep.tile([P, width], U32, name=name + "_codes", tag=tag or name, align_bytes=64)
             scales = keep.tile([P, width], U8, name=name + "_scales", align_bytes=64)
             c = 0
             for step in widths:
@@ -73,28 +78,26 @@ def tile_attend_gsq_pl_nag_kernel(tc, xT, wT, y, wt, xm, mT, offs, out_0, out_1,
         for u in range(2):
             nc.sync.dma_start(target_pairs[u][:], y_rows[:, 2 * u : 2 * u + 2, :])
         target = [target_pairs[j // 2][:, j % 2, :] for j in range(L)]
-        xm_raw = keep.tile([P, L, D], F32, name="xm_raw", tag="late")
+        xm_raw = keep.tile([P, L, D], F32, name="xm_raw")
         nc.sync.dma_start(xm_raw[:], xm_rows)
-        m_src = [keep.tile([P, T], F32, name=f"m_src{j}", tag=f"m_src{j}") for j in range(L)]
+        m_src = [keep.tile([P, T], F32, name=f"m_src{j}") for j in range(L)]
         for j in range(L):
             nc.sync.dma_start(m_src[j][:], m_planes[:, j, :])
+        w_new = [keep.tile([P, T], F32, name=f"w_new{j}") for j in range(L)]
+        nc.sync.dma_start(w_new[L - 1][:], w_planes[:, L - 1, :])
 
-        identity = keep.tile([P, P], F32, name="identity", tag="terms")
-        make_identity(nc, identity[:])
         w_got = keep.tile([P, L, N], F32, name="w_got")
-        w_new = []
         w_bf = keep.tile([P, L * N], BF16, name="w_bf", align_bytes=64)
-        halves = [slice(0, N // 2), slice(N // 2, N)]
         for j in range(L):
-            parts = halves if j == L - 1 else [slice(0, N)]
-            for part in parts:
-                nc.vector.tensor_copy(w_got[:, j, part], w_src[j][:].indirect(offsets[:, part.start // 16 : part.stop // 16]))
-            if j % 2 == 1:
-                for part in parts:
-                    nc.vector.tensor_copy(w_bf[:].rearrange("p (n t) -> p n t", t=L)[:, part, j - 1 : j + 1], w_got[:, j - 1 : j + 1, part].rearrange("p t n -> p n t"))
             if j < L - 1:
-                w_new.append(keep.tile([P, T], F32, name=f"w_new{j}"))
+                nc.vector.tensor_copy(w_got[:, j, :], listed(w_src[j], whole[0]))
                 nc.scalar.activation(w_new[j][:], w_src[j][:], COPY)
+            else:
+                nc.vector.tensor_copy(w_got[:, j, halves[0]], listed(w_src[j], halves[0]))
+                nc.scalar.activation(w_got[:, j, halves[1]], listed(w_src[j], halves[1]), COPY)
+            if j % 2 == 1:
+                for part, copy in zip(halves, (nc.vector.tensor_copy, nc.scalar.copy)) if j == L - 1 else [(whole[0], nc.vector.tensor_copy)]:
+                    copy(w_bf[:].rearrange("p (n t) -> p n t", t=L)[:, part, j - 1 : j + 1], w_got[:, j - 1 : j + 1, part].rearrange("p t n -> p n t"))
         w_codes, w_scales = quantise("w", w_bf, E4M3, (256, 256))
         x_bf = keep.tile([P, L * R], BF16, name="x_bf", align_bytes=64)
         deal(x_bf, x_raw, slice(0, 2), nc.vector.tensor_copy)
@@ -108,114 +111,81 @@ def tile_attend_gsq_pl_nag_kernel(tc, xT, wT, y, wt, xm, mT, offs, out_0, out_1,
                 nc.vector.tensor_scalar_mul(target[j], target[j], weight[:, j : j + 1])
             else:
                 nc.scalar.activation(target[j], target[j], COPY, scale=weight[:, j : j + 1])
-            if j == 0:
-                for h, part in enumerate(halves):
-                    score = psum.tile([P, N], F32, name=f"score0_{h}", tag=("score0", "grad3")[h])
-                    nc.tensor.matmul_mx(out=score[:, part], lhsT=x_codes[:, cols].bitcast(E4M3), lhsT_scale=x_scales[:, cols], rhs=w_codes[:, part].bitcast(E4M3), rhs_scale=w_scales[:, part], start=True, stop=True)
+            for h, product in enumerate(halves if j == 0 else whole):
+                score = psum.tile([P, N], F32, name=f"score{j}_{h}", tag=f"score{j}" if h == 0 else "grad3")
+                nc.tensor.matmul_mx(out=score[:, product], lhsT=x_codes[:, cols].bitcast(E4M3), lhsT_scale=x_scales[:, cols], rhs=w_codes[:, product].bitcast(E4M3), rhs_scale=w_scales[:, product], start=True, stop=True)
+                for part in halves if j == L - 1 else [product]:
                     nc.vector.scalar_tensor_tensor(g_flat[:, j, part], score[:, part], weight[:, j : j + 1], target[j][:, part], MULT, SUB)
-            else:
-                score = psum.tile([P, N], F32, name=f"score{j}", tag=f"score{j}")
-                nc.tensor.matmul_mx(out=score[:], lhsT=x_codes[:, cols].bitcast(E4M3), lhsT_scale=x_scales[:, cols], rhs=w_codes[:].bitcast(E4M3), rhs_scale=w_scales[:], start=True, stop=True)
-                for part in halves if j == L - 1 else [slice(0, N)]:
-                    nc.vector.scalar_tensor_tensor(g_flat[:, j, part], score[:, part], weight[:, j : j + 1], target[j][:, part], MULT, SUB)
-        g_bf = keep.tile([P, L * N], BF16, name="g_bf", tag="g_bf", align_bytes=64)
+        g_bf = keep.tile([P, L * N], BF16, name="g_bf", align_bytes=64)
         for part in halves:
             weave(g_bf[:, L * part.start : L * part.stop], g_flat[:, :, part])
-        xm_bf = keep.tile([P, L * D], BF16, name="xm_bf", tag="xm_bf", align_bytes=64)
+        xm_bf = keep.tile([P, L * D], BF16, name="xm_bf", align_bytes=64)
         deal(xm_bf, xm_raw, slice(0, 2), nc.scalar.copy)
         deal(xm_bf, xm_raw, slice(2, 4), nc.scalar.copy)
         g_codes, g_scales = quantise("g", g_bf, E5M2, (256, 256))
-        xm_codes, xm_scales = quantise("xm", xm_bf, E4M3, (256, 256))
 
         grad = []
+
+        def gradient_pair(u):
+            xm_codes, xm_scales = quantise(f"xm{u}", xm_bf[:, 2 * u * D : 2 * (u + 1) * D], E4M3, (256,), tag="first" if u == 1 else None)
+            for j in (2 * u, 2 * u + 1):
+                cols = slice((j % 2) * P, (j % 2 + 1) * P)
+                grad.append(psum.tile([P, N], F32, name=f"grad{j}", tag=f"grad{j}"))
+                nc.tensor.matmul_mx(out=grad[j][:], lhsT=xm_codes[:, cols].bitcast(E4M3), lhsT_scale=xm_scales[:, cols], rhs=g_codes[:].bitcast(E5M2), rhs_scale=g_scales[:], start=True, stop=True)
+
+        gradient_pair(0)
+
+        m_step = [keep.tile([P, N], F32, name=f"m_step{j}", tag="pairs" if j == L - 1 else f"m_step{j}") for j in range(L)]
+        m_val = keep.tile([P, L, N], F32, name="m_val")
+        ahead = [keep.tile([P, N], F32, name=f"ahead{j}", tag=("first", "ahead1", "ahead2", "late")[j], align_bytes=64) for j in range(L)]
+        m_new = [keep.tile([P, T], F32, name=f"m_new{j}", tag="late" if j == 2 else f"table{j}", align_bytes=64 if j == 2 else None) for j in range(L)]
+        nc.sync.dma_start(m_new[L - 1][:], m_planes[:, L - 1, :])
+
+        def scatter_on_scalar(window, values, part):
+            nc.scalar.activation(listed(window, part), values[:, part], COPY)
+
+        def momentum(j, part):
+            nc.vector.scalar_tensor_tensor(m_val[:, j, part], m_step[j][:, part], BETA / MOM_STEP, grad[j][:, part], MULT, ADD)
+
         for j in range(L):
-            cols = slice(j * P, (j + 1) * P)
-            grad.append(psum.tile([P, N], F32, name=f"grad{j}", tag=f"grad{j}"))
-            nc.tensor.matmul_mx(out=grad[j][:], lhsT=xm_codes[:, cols].bitcast(E4M3), lhsT_scale=xm_scales[:, cols], rhs=g_codes[:].bitcast(E5M2), rhs_scale=g_scales[:], start=True, stop=True)
-        w_new.append(keep.tile([P, T], F32, name="w_new3", tag="late"))
-        nc.scalar.activation(w_new[L - 1][:], w_src[L - 1][:], COPY)
+            nc.vector.tensor_scalar(m_step[j][:], listed(m_src[j], whole[0]), MOM_STEP, 0.0, MULT, ADD)
+            if j == 0:
+                nc.scalar.activation(m_new[j][:], m_src[j][:], COPY)
+            if j == 1:
+                nc.vector.tensor_copy(m_new[j][:], m_src[j][:])
+            if j != 2:
+                for part in halves:
+                    nc.vector.tensor_tensor(ahead[j][:, part], w_got[:, j, part], m_step[j][:, part], ADD)
+                for part in halves:
+                    nc.vector.scalar_tensor_tensor(w_got[:, j, part], grad[j][:, part], GRAD_STEP, ahead[j][:, part], MULT, ADD)
+                    scatter_on_scalar(w_new[j], w_got[:, j, :], part)
+                    momentum(j, part)
+                    scatter_on_scalar(m_new[j], m_val[:, j, :], part)
+            else:
+                nc.vector.scalar_tensor_tensor(ahead[j][:], grad[j][:], GRAD_STEP, m_step[j][:], MULT, ADD)
+                momentum(j, whole[0])
+                nc.vector.tensor_tensor(listed(w_new[j], whole[0]), ahead[j][:], w_got[:, j, :], ADD)
+            if j == 0:
+                gradient_pair(1)
+        nc.vector.tensor_copy(m_new[2][:], m_src[2][:])
+        for part in halves:
+            scatter_on_scalar(m_new[2], m_val[:, 2, :], part)
+        for planes, tables, j in ((o0_planes, w_new, 0), (o1_planes, m_new, 0), (o0_planes, w_new, 2), (o0_planes, w_new, 1), (o1_planes, m_new, 1), (o0_planes, w_new, 3), (o1_planes, m_new, 2)):
+            nc.sync.dma_start(planes[:, j, :], tables[j][:])
 
-        m_new = [keep.tile([P, T], F32, name=f"m_new{j}", tag=f"table{j}") for j in range(L)]
-        for j in range(L):
-            nc.sync.dma_start(m_new[j][:], m_planes[:, j, :])
-
-        m_first = keep.tile([P, N], F32, name="m_first", tag="g_bf", align_bytes=64)
-        m_rest = keep.tile([P, L - 1, N], F32, name="m_rest")
-        m_step = [m_first[:]] + [m_rest[:, j, :] for j in range(L - 1)]
-
-        def gather_m(j):
-            nc.vector.tensor_scalar(m_step[j], m_src[j][:].indirect(offsets[:]), -LR * BETA * BETA, 0.0, MULT, ADD)
-
-        def put_w(j):
-            nc.vector.tensor_tensor(w_new[j][:].indirect(offsets[:]), descended[j], m_step[j], ADD)
-            nc.sync.dma_start(o0_planes[:, j, :], w_new[j][:])
-
-        def round_plane(j):
-            nc.scalar.copy(pairs[:, j // 2, :, j % 2], w_new[j][:])
-
-        def momentum_terms(j):
-            nc.scalar.activation(dw[:, j, :], grad[j][:], COPY)
-            nc.scalar.activation(kept[j], m_step[j], COPY, scale=-1.0 / (LR * BETA))
-
-        def put_m(j):
-            nc.vector.tensor_tensor(m_new[j][:].indirect(offsets[:]), kept[j], dw[:, j, :], ADD)
-            nc.sync.dma_start(o1_planes[:, j, :], m_new[j][:])
-
-        gather_m(0)
-        first = keep.tile([P, N], F32, name="first", tag="m_src0")
-        descended = [first[:]] + [w_got[:, j, :] for j in range(1, L)]
-        nc.vector.scalar_tensor_tensor(first[:], grad[0][:], -LR * (1.0 + BETA), w_got[:, 0, :], MULT, ADD)
-        put_w(0)
-
-        dw_step = keep.tile([P, L - 1, N], F32, name="dw_step", tag="dw_step")
-        turned = keep.tile([P, L - 1, N], F32, name="turned", tag="pairs")
-        for j in range(1, L):
-            nc.scalar.activation(dw_step[:, j - 1, :], grad[j][:], COPY, scale=-LR * (1.0 + BETA))
-        for j in range(1, L):
-            there = psum.tile([P, N], F32, name=f"there{j}", tag=f"score{j}")
-            for c in range(N // P):
-                cols = slice(c * P, (c + 1) * P)
-                nc.tensor.matmul(there[:, cols], w_got[:, j, cols], identity[:], start=True, stop=False, is_transpose=True)
-                nc.tensor.matmul(there[:, cols], dw_step[:, j - 1, cols], identity[:], start=False, stop=True, is_transpose=True)
-            nc.scalar.copy(turned[:, j - 1, :], there[:])
-        back = {}
-        for j in range(1, L):
-            back[j] = psum.tile([P, N], F32, name=f"back{j}", tag=f"score{j}")
-            for c in range(N // P):
-                cols = slice(c * P, (c + 1) * P)
-                nc.tensor.transpose(back[j][:, cols], turned[:, j - 1, cols], identity[:])
-            nc.scalar.copy(descended[j], back[j][:])
         pairs = keep.tile([P, 2, T, 2], BF16, name="pairs", tag="pairs")
-        round_plane(0)
-        terms = keep.tile([P, 2 * L - 1, N], F32, name="terms", tag="terms")
-        dw = terms[:, :L, :]
-        kept = [terms[:, L + j, :] for j in range(L - 1)]
-        momentum_terms(0)
-
-        for j in range(1, L):
-            gather_m(j)
-        for j in range(1, L):
-            put_w(j)
-        for j in range(1, L - 1):
-            momentum_terms(j)
-            round_plane(j)
-        round_plane(L - 1)
-
-        for j in range(L - 1):
-            put_m(j)
+        for j in range(L):
+            nc.vector.tensor_copy(pairs[:, j // 2, :, j % 2], w_new[j][:])
+        pair_words = pairs[:].rearrange("p u n e -> p u (n e)").bitcast(I32)
         out_scales = keep.tile([P, T], U8, name="out_scales", align_bytes=64)
-        out_bf = [keep.tile([P, L * T // 2], BF16, name=f"out_bf{h}", align_bytes=64) for h in range(2)]
-        pair_words = pairs[:].rearrange("p u n e -> p u (n e)").bitcast(F32)
-        for h in range(2):
-            nc.scalar.copy(out_bf[h][:].bitcast(F32).rearrange("p (n u) -> p n u", u=2), pair_words[:, :, h * T // 2 : (h + 1) * T // 2].rearrange("p u n -> p n u"))
-        for h in range(2):
-            cols = slice(h * T // 2, (h + 1) * T // 2)
-            out_codes = keep.tile([P, T // 2], U32, name=f"out_codes{h}", align_bytes=64)
-            nc.vector.quantize_mx(out=out_codes[:].bitcast(E4M3), scales=out_scales[:, cols], in_=out_bf[h][:])
+        for q, cols in enumerate((slice(0, T // 2), slice(T // 2, 3 * T // 4), slice(3 * T // 4, T))):
+            width = cols.stop - cols.start
+            out_bf = keep.tile([P, L * width], BF16, name=f"out_bf{q}", align_bytes=64)
+            nc.vector.tensor_copy(out_bf[:].bitcast(I32).rearrange("p (n u) -> p n u", u=2), pair_words[:, :, cols].rearrange("p u n -> p n u"))
+            out_codes = keep.tile([P, width], U32, name=f"out_codes{q}", align_bytes=64)
+            nc.vector.quantize_mx(out=out_codes[:].bitcast(E4M3), scales=out_scales[:, cols], in_=out_bf[:])
             nc.sync.dma_start(words_out[:, cols], out_codes[:].bitcast(I32))
-        for q in range(4):
-            nc.sync.dma_start(scales_out[4 * q : 4 * q + 4, :], out_scales[32 * q : 32 * q + 4, :].bitcast(I32))
-        kept_last = keep.tile([P, N], F32, name="kept_last", tag="pairs")
-        kept.append(kept_last[:])
-        momentum_terms(L - 1)
-        put_m(L - 1)
+            if q == 0:
+                nc.sync.dma_start(o1_planes[:, 3, :], m_new[3][:])
+        for f in range(4):
+            nc.sync.dma_start(scales_out[4 * f : 4 * f + 4, :], out_scales[32 * f : 32 * f + 4, :].bitcast(I32))

@@ -107,10 +107,7 @@ def tile_attend_gsq_pl_nag_kernel(tc, xT, wT, y, wt, xm, mT, offs, out_0, out_1,
         g_flat = keep.tile([P, L, N], BF16, name="g_flat")
         for j in range(L):
             cols = slice(j * P, (j + 1) * P)
-            if j == 0:
-                nc.vector.tensor_scalar_mul(target[j], target[j], weight[:, j : j + 1])
-            else:
-                nc.scalar.activation(target[j], target[j], COPY, scale=weight[:, j : j + 1])
+            nc.scalar.activation(target[j], target[j], COPY, scale=weight[:, j : j + 1])
             for h, product in enumerate(halves if j == 0 else whole):
                 score = psum.tile([P, N], F32, name=f"score{j}_{h}", tag=f"score{j}" if h == 0 else "grad3")
                 nc.tensor.matmul_mx(out=score[:, product], lhsT=x_codes[:, cols].bitcast(E4M3), lhsT_scale=x_scales[:, cols], rhs=w_codes[:, product].bitcast(E4M3), rhs_scale=w_scales[:, product], start=True, stop=True)
@@ -121,19 +118,20 @@ def tile_attend_gsq_pl_nag_kernel(tc, xT, wT, y, wt, xm, mT, offs, out_0, out_1,
             weave(g_bf[:, L * part.start : L * part.stop], g_flat[:, :, part])
         xm_bf = keep.tile([P, L * D], BF16, name="xm_bf", align_bytes=64)
         deal(xm_bf, xm_raw, slice(0, 2), nc.scalar.copy)
-        deal(xm_bf, xm_raw, slice(2, 4), nc.scalar.copy)
         g_codes, g_scales = quantise("g", g_bf, E5M2, (256, 256))
 
         grad = []
 
         def gradient_pair(u):
-            xm_codes, xm_scales = quantise(f"xm{u}", xm_bf[:, 2 * u * D : 2 * (u + 1) * D], E4M3, (256,), tag="first" if u == 1 else None)
+            xm_codes, xm_scales = quantise(f"xm{u}", xm_bf[:, 2 * u * D : 2 * (u + 1) * D], E4M3, (256,), tag=None)
             for j in (2 * u, 2 * u + 1):
                 cols = slice((j % 2) * P, (j % 2 + 1) * P)
                 grad.append(psum.tile([P, N], F32, name=f"grad{j}", tag=f"grad{j}"))
                 nc.tensor.matmul_mx(out=grad[j][:], lhsT=xm_codes[:, cols].bitcast(E4M3), lhsT_scale=xm_scales[:, cols], rhs=g_codes[:].bitcast(E5M2), rhs_scale=g_scales[:], start=True, stop=True)
 
         gradient_pair(0)
+        deal(xm_bf, xm_raw, slice(2, 4), nc.vector.tensor_copy)
+        gradient_pair(1)
 
         m_step = [keep.tile([P, N], F32, name=f"m_step{j}", tag="pairs" if j == L - 1 else f"m_step{j}") for j in range(L)]
         m_val = keep.tile([P, L, N], F32, name="m_val")
@@ -148,8 +146,10 @@ def tile_attend_gsq_pl_nag_kernel(tc, xT, wT, y, wt, xm, mT, offs, out_0, out_1,
             nc.vector.scalar_tensor_tensor(m_val[:, j, part], m_step[j][:, part], BETA / MOM_STEP, grad[j][:, part], MULT, ADD)
 
         for j in range(L):
-            nc.vector.tensor_scalar(m_step[j][:], listed(m_src[j], whole[0]), MOM_STEP, 0.0, MULT, ADD)
+            if j > 0:
+                nc.vector.tensor_scalar(m_step[j][:], listed(m_src[j], whole[0]), MOM_STEP, 0.0, MULT, ADD)
             if j == 0:
+                nc.scalar.activation(m_step[j][:], listed(m_src[j], whole[0]), COPY, scale=MOM_STEP)
                 nc.scalar.activation(m_new[j][:], m_src[j][:], COPY)
             if j == 1:
                 nc.vector.tensor_copy(m_new[j][:], m_src[j][:])
@@ -165,8 +165,6 @@ def tile_attend_gsq_pl_nag_kernel(tc, xT, wT, y, wt, xm, mT, offs, out_0, out_1,
                 nc.vector.scalar_tensor_tensor(ahead[j][:], grad[j][:], GRAD_STEP, m_step[j][:], MULT, ADD)
                 momentum(j, whole[0])
                 nc.vector.tensor_tensor(listed(w_new[j], whole[0]), ahead[j][:], w_got[:, j, :], ADD)
-            if j == 0:
-                gradient_pair(1)
         nc.vector.tensor_copy(m_new[2][:], m_src[2][:])
         for part in halves:
             scatter_on_scalar(m_new[2], m_val[:, 2, :], part)
@@ -177,15 +175,19 @@ def tile_attend_gsq_pl_nag_kernel(tc, xT, wT, y, wt, xm, mT, offs, out_0, out_1,
         for j in range(L):
             nc.vector.tensor_copy(pairs[:, j // 2, :, j % 2], w_new[j][:])
         pair_words = pairs[:].rearrange("p u n e -> p u (n e)").bitcast(I32)
-        out_scales = keep.tile([P, T], U8, name="out_scales", align_bytes=64)
-        for q, cols in enumerate((slice(0, T // 2), slice(T // 2, 3 * T // 4), slice(3 * T // 4, T))):
-            width = cols.stop - cols.start
-            out_bf = keep.tile([P, L * width], BF16, name=f"out_bf{q}", align_bytes=64)
+        quarter = T // 4
+        out_scales = keep.tile([P, quarter], U8, name="out_scales", align_bytes=64)
+        out_codes = [keep.tile([P, width], U32, name=f"out_codes{k}", align_bytes=64) for k, width in enumerate((2 * quarter, quarter, quarter))]
+        code_cols = [out_codes[0][:, :quarter], out_codes[0][:, quarter:], out_codes[1][:], out_codes[2][:]]
+        for q in range(4):
+            cols = slice(q * quarter, (q + 1) * quarter)
+            out_bf = keep.tile([P, L * quarter], BF16, name=f"out_bf{q}", align_bytes=64)
             nc.vector.tensor_copy(out_bf[:].bitcast(I32).rearrange("p (n u) -> p n u", u=2), pair_words[:, :, cols].rearrange("p u n -> p n u"))
-            out_codes = keep.tile([P, width], U32, name=f"out_codes{q}", align_bytes=64)
-            nc.vector.quantize_mx(out=out_codes[:].bitcast(E4M3), scales=out_scales[:, cols], in_=out_bf[:])
-            nc.sync.dma_start(words_out[:, cols], out_codes[:].bitcast(I32))
-            if q == 0:
+            nc.vector.quantize_mx(out=code_cols[q].bitcast(E4M3), scales=out_scales[4 * q :, :], in_=out_bf[:])
+            if q > 0:
+                done = slice(0, cols.stop) if q == 1 else cols
+                nc.sync.dma_start(words_out[:, done], out_codes[q - 1][:].bitcast(I32))
+            if q == 1:
                 nc.sync.dma_start(o1_planes[:, 3, :], m_new[3][:])
         for f in range(4):
-            nc.sync.dma_start(scales_out[4 * f : 4 * f + 4, :], out_scales[32 * f : 32 * f + 4, :].bitcast(I32))
+            nc.sync.dma_start(scales_out[4 * f : 4 * f + 4, :].rearrange("i (q c) -> q i c", q=4), out_scales[32 * f : 32 * f + 16, :].bitcast(I32))

@@ -81,10 +81,11 @@ def tile_attend_gsq_pl_nag_kernel(tc, xT, wT, y, wt, xm, mT, offs, out_0, out_1,
         xm_raw = keep.tile([P, L, D], F32, name="xm_raw")
         nc.sync.dma_start(xm_raw[:], xm_rows)
         m_src = [keep.tile([P, T], F32, name=f"m_src{j}") for j in range(L)]
-        for j in range(L):
-            nc.sync.dma_start(m_src[j][:], m_planes[:, j, :])
         w_new = [keep.tile([P, T], F32, name=f"w_new{j}") for j in range(L)]
-        nc.sync.dma_start(w_new[L - 1][:], w_planes[:, L - 1, :])
+        for j in range(L):
+            if j == L - 1:
+                nc.sync.dma_start(w_new[j][:], w_planes[:, j, :])
+            nc.sync.dma_start(m_src[j][:], m_planes[:, j, :])
 
         w_got = keep.tile([P, L, N], F32, name="w_got")
         w_bf = keep.tile([P, L * N], BF16, name="w_bf", align_bytes=64)
@@ -133,48 +134,57 @@ def tile_attend_gsq_pl_nag_kernel(tc, xT, wT, y, wt, xm, mT, offs, out_0, out_1,
         deal(xm_bf, xm_raw, slice(2, 4), nc.vector.tensor_copy)
         gradient_pair(1)
 
-        m_step = [keep.tile([P, N], F32, name=f"m_step{j}", tag="pairs" if j == L - 1 else f"m_step{j}") for j in range(L)]
+        flat = keep.tile([P, L * T], BF16, name="rounded")
+        rounded = flat[:].rearrange("p (j t) -> p j t", j=L)
         m_val = keep.tile([P, L, N], F32, name="m_val")
-        ahead = [keep.tile([P, N], F32, name=f"ahead{j}", tag=("first", "ahead1", "ahead2", "late")[j], align_bytes=64) for j in range(L)]
-        m_new = [keep.tile([P, T], F32, name=f"m_new{j}", tag="late" if j == 2 else f"table{j}", align_bytes=64 if j == 2 else None) for j in range(L)]
+        steps = [keep.tile([P, N], F32, name=f"m_step{j}", tag="late" if j == 2 else f"m_step{j}")[:] for j in range(L - 1)] + [m_val[:, 2, :]]
+        m_step = [[step[:, part] for part in halves] for step in steps]
+        ahead = [keep.tile([P, N], F32, name=f"ahead{j}", tag=f"ahead{j}") for j in range(L - 1)]
+        m_new = [keep.tile([P, T], F32, name=f"m_new{j}", tag="late" if j == 2 else f"table{j}") for j in range(L)]
         nc.sync.dma_start(m_new[L - 1][:], m_planes[:, L - 1, :])
 
         def scatter_on_scalar(window, values, part):
             nc.scalar.activation(listed(window, part), values[:, part], COPY)
 
-        def momentum(j, part):
-            nc.vector.scalar_tensor_tensor(m_val[:, j, part], m_step[j][:, part], BETA / MOM_STEP, grad[j][:, part], MULT, ADD)
+        def momentum(j, part, step):
+            nc.vector.scalar_tensor_tensor(m_val[:, j, part], step, BETA / MOM_STEP, grad[j][:, part], MULT, ADD)
 
         for j in range(L):
             if j > 0:
-                nc.vector.tensor_scalar(m_step[j][:], listed(m_src[j], whole[0]), MOM_STEP, 0.0, MULT, ADD)
+                nc.vector.tensor_scalar(steps[j][:], listed(m_src[j], whole[0]), MOM_STEP, 0.0, MULT, ADD)
             if j == 0:
-                nc.scalar.activation(m_step[j][:], listed(m_src[j], whole[0]), COPY, scale=MOM_STEP)
+                nc.scalar.activation(steps[j][:], listed(m_src[j], whole[0]), COPY, scale=MOM_STEP)
                 nc.scalar.activation(m_new[j][:], m_src[j][:], COPY)
             if j == 1:
                 nc.vector.tensor_copy(m_new[j][:], m_src[j][:])
             if j != 2:
-                for part in halves:
-                    nc.vector.tensor_tensor(ahead[j][:, part], w_got[:, j, part], m_step[j][:, part], ADD)
-                for part in halves:
-                    nc.vector.scalar_tensor_tensor(w_got[:, j, part], grad[j][:, part], GRAD_STEP, ahead[j][:, part], MULT, ADD)
+                sums = [flat[:, T : T + N].bitcast(F32), m_val[:, 1, halves[1]]] if j == L - 1 else [ahead[j][:, part] for part in halves]
+                for part, total, step in zip(halves, sums, m_step[j]):
+                    nc.vector.tensor_tensor(total, w_got[:, j, part], step, ADD)
+                for h, part in enumerate(halves):
+                    nc.vector.scalar_tensor_tensor(w_got[:, j, part], grad[j][:, part], GRAD_STEP, sums[h], MULT, ADD)
                     scatter_on_scalar(w_new[j], w_got[:, j, :], part)
-                    momentum(j, part)
-                    scatter_on_scalar(m_new[j], m_val[:, j, :], part)
+                    if (j, h) == (L - 1, 1):
+                        momentum(1, part, m_step[1][h])
+                        scatter_on_scalar(m_new[1], m_val[:, 1, :], part)
+                    if (j, h) != (1, 1):
+                        momentum(j, part, m_step[j][h])
+                        scatter_on_scalar(m_new[j], m_val[:, j, :], part)
             else:
-                nc.vector.scalar_tensor_tensor(ahead[j][:], grad[j][:], GRAD_STEP, m_step[j][:], MULT, ADD)
-                momentum(j, whole[0])
+                nc.vector.scalar_tensor_tensor(ahead[j][:], grad[j][:], GRAD_STEP, steps[j][:], MULT, ADD)
                 nc.vector.tensor_tensor(listed(w_new[j], whole[0]), ahead[j][:], w_got[:, j, :], ADD)
+        momentum(2, whole[0], steps[2][:])
         nc.vector.tensor_copy(m_new[2][:], m_src[2][:])
         for part in halves:
             scatter_on_scalar(m_new[2], m_val[:, 2, :], part)
-        for planes, tables, j in ((o0_planes, w_new, 0), (o1_planes, m_new, 0), (o0_planes, w_new, 2), (o0_planes, w_new, 1), (o1_planes, m_new, 1), (o0_planes, w_new, 3), (o1_planes, m_new, 2)):
+        for planes, tables, j in ((o0_planes, w_new, 0), (o1_planes, m_new, 0), (o0_planes, w_new, 2), (o0_planes, w_new, 1), (o0_planes, w_new, 3), (o1_planes, m_new, 1), (o1_planes, m_new, 3)):
             nc.sync.dma_start(planes[:, j, :], tables[j][:])
 
-        pairs = keep.tile([P, 2, T, 2], BF16, name="pairs", tag="pairs")
-        for j in range(L):
-            nc.vector.tensor_copy(pairs[:, j // 2, :, j % 2], w_new[j][:])
-        pair_words = pairs[:].rearrange("p u n e -> p u (n e)").bitcast(I32)
+        for j in (0, 2):
+            for part in (slice(0, T // 2), slice(T // 2, T)):
+                nc.gpsimd.tensor_copy(rounded[:, j, part], w_new[j][:, part])
+        for j in (1, 3):
+            nc.vector.tensor_copy(rounded[:, j, :], w_new[j][:])
         quarter = T // 4
         out_scales = keep.tile([P, quarter], U8, name="out_scales", align_bytes=64)
         out_codes = [keep.tile([P, width], U32, name=f"out_codes{k}", align_bytes=64) for k, width in enumerate((2 * quarter, quarter, quarter))]
@@ -182,12 +192,12 @@ def tile_attend_gsq_pl_nag_kernel(tc, xT, wT, y, wt, xm, mT, offs, out_0, out_1,
         for q in range(4):
             cols = slice(q * quarter, (q + 1) * quarter)
             out_bf = keep.tile([P, L * quarter], BF16, name=f"out_bf{q}", align_bytes=64)
-            nc.vector.tensor_copy(out_bf[:].bitcast(I32).rearrange("p (n u) -> p n u", u=2), pair_words[:, :, cols].rearrange("p u n -> p n u"))
+            weave(out_bf[:], rounded[:, :, cols])
             nc.vector.quantize_mx(out=code_cols[q].bitcast(E4M3), scales=out_scales[4 * q :, :], in_=out_bf[:])
             if q > 0:
                 done = slice(0, cols.stop) if q == 1 else cols
                 nc.sync.dma_start(words_out[:, done], out_codes[q - 1][:].bitcast(I32))
             if q == 1:
-                nc.sync.dma_start(o1_planes[:, 3, :], m_new[3][:])
+                nc.sync.dma_start(o1_planes[:, 2, :], m_new[2][:])
         for f in range(4):
             nc.sync.dma_start(scales_out[4 * f : 4 * f + 4, :].rearrange("i (q c) -> q i c", q=4), out_scales[32 * f : 32 * f + 16, :].bitcast(I32))

@@ -74,17 +74,16 @@ def tile_attend_gsq_pl_nag_kernel(tc, xT, wT, y, wt, xm, mT, offs, out_0, out_1,
         nc.sync.dma_start(x_raw[:], x_rows)
         weight = keep.tile([P, L], F32, name="weight")
         nc.sync.dma_start(weight[:], wt[0].rearrange("(p j) o -> p (j o)", j=L))
-        target_pairs = [keep.tile([P, 2, N], F32, name=f"target{u}") for u in range(2)]
+        target_pairs = [keep.tile([P, 2, N], F32, name=f"target{u}", tag=f"y{u}") for u in range(2)]
         for u in range(2):
             nc.sync.dma_start(target_pairs[u][:], y_rows[:, 2 * u : 2 * u + 2, :])
-        target = [target_pairs[j // 2][:, j % 2, :] for j in range(L)]
+        scaled = keep.tile([P, 2, N], F32, name="scaled")
+        target = [scaled[:, 0, :], scaled[:, 1, :], target_pairs[1][:, 0, :], target_pairs[1][:, 1, :]]
         xm_raw = keep.tile([P, L, D], F32, name="xm_raw")
         nc.sync.dma_start(xm_raw[:], xm_rows)
         m_src = [keep.tile([P, T], F32, name=f"m_src{j}") for j in range(L)]
-        w_new = [keep.tile([P, T], F32, name=f"w_new{j}") for j in range(L)]
+        w_new = [keep.tile([P, T], F32, name=f"w_new{j}") for j in range(L - 1)]
         for j in range(L):
-            if j == L - 1:
-                nc.sync.dma_start(w_new[j][:], w_planes[:, j, :])
             nc.sync.dma_start(m_src[j][:], m_planes[:, j, :])
 
         w_got = keep.tile([P, L, N], F32, name="w_got")
@@ -108,12 +107,17 @@ def tile_attend_gsq_pl_nag_kernel(tc, xT, wT, y, wt, xm, mT, offs, out_0, out_1,
         g_flat = keep.tile([P, L, N], BF16, name="g_flat")
         for j in range(L):
             cols = slice(j * P, (j + 1) * P)
-            nc.scalar.activation(target[j], target[j], COPY, scale=weight[:, j : j + 1])
+            if j < 2:
+                nc.scalar.activation(target[j], target_pairs[0][:, j, :], COPY, scale=weight[:, j : j + 1])
+            else:
+                nc.gpsimd.tensor_scalar(target[j], target[j], weight[:, j : j + 1], 0.0, MULT, ADD)
             for h, product in enumerate(halves if j == 0 else whole):
                 score = psum.tile([P, N], F32, name=f"score{j}_{h}", tag=f"score{j}" if h == 0 else "grad3")
                 nc.tensor.matmul_mx(out=score[:, product], lhsT=x_codes[:, cols].bitcast(E4M3), lhsT_scale=x_scales[:, cols], rhs=w_codes[:, product].bitcast(E4M3), rhs_scale=w_scales[:, product], start=True, stop=True)
                 for part in halves if j == L - 1 else [product]:
                     nc.vector.scalar_tensor_tensor(g_flat[:, j, part], score[:, part], weight[:, j : j + 1], target[j][:, part], MULT, SUB)
+        w_new.append(keep.tile([P, T], F32, name="w_new3", tag="y0"))
+        nc.scalar.activation(w_new[L - 1][:], w_src[L - 1][:], COPY)
         g_bf = keep.tile([P, L * N], BF16, name="g_bf", align_bytes=64)
         for part in halves:
             weave(g_bf[:, L * part.start : L * part.stop], g_flat[:, :, part])
@@ -137,11 +141,12 @@ def tile_attend_gsq_pl_nag_kernel(tc, xT, wT, y, wt, xm, mT, offs, out_0, out_1,
         flat = keep.tile([P, L * T], BF16, name="rounded")
         rounded = flat[:].rearrange("p (j t) -> p j t", j=L)
         m_val = keep.tile([P, L, N], F32, name="m_val")
-        steps = [keep.tile([P, N], F32, name=f"m_step{j}", tag="late" if j == 2 else f"m_step{j}")[:] for j in range(L - 1)] + [m_val[:, 2, :]]
+        steps = [keep.tile([P, N], F32, name=f"m_step{j}", tag=f"m_step{j}")[:] for j in range(L - 1)] + [m_val[:, 2, :]]
         m_step = [[step[:, part] for part in halves] for step in steps]
         ahead = [keep.tile([P, N], F32, name=f"ahead{j}", tag=f"ahead{j}") for j in range(L - 1)]
-        m_new = [keep.tile([P, T], F32, name=f"m_new{j}", tag="late" if j == 2 else f"table{j}") for j in range(L)]
-        nc.sync.dma_start(m_new[L - 1][:], m_planes[:, L - 1, :])
+        m_new = [keep.tile([P, T], F32, name=f"m_new{j}", tag=f"table{j}") for j in range(L)]
+        for j in (3, 2):
+            nc.sync.dma_start(m_new[j][:], m_planes[:, j, :])
 
         def scatter_on_scalar(window, values, part):
             nc.scalar.activation(listed(window, part), values[:, part], COPY)
@@ -166,7 +171,7 @@ def tile_attend_gsq_pl_nag_kernel(tc, xT, wT, y, wt, xm, mT, offs, out_0, out_1,
                     scatter_on_scalar(w_new[j], w_got[:, j, :], part)
                     if (j, h) == (L - 1, 1):
                         momentum(1, part, m_step[1][h])
-                        scatter_on_scalar(m_new[1], m_val[:, 1, :], part)
+                        nc.vector.tensor_copy(listed(m_new[1], part), m_val[:, 1, part])
                     if (j, h) != (1, 1):
                         momentum(j, part, m_step[j][h])
                         scatter_on_scalar(m_new[j], m_val[:, j, :], part)
@@ -174,7 +179,6 @@ def tile_attend_gsq_pl_nag_kernel(tc, xT, wT, y, wt, xm, mT, offs, out_0, out_1,
                 nc.vector.scalar_tensor_tensor(ahead[j][:], grad[j][:], GRAD_STEP, steps[j][:], MULT, ADD)
                 nc.vector.tensor_tensor(listed(w_new[j], whole[0]), ahead[j][:], w_got[:, j, :], ADD)
         momentum(2, whole[0], steps[2][:])
-        nc.vector.tensor_copy(m_new[2][:], m_src[2][:])
         for part in halves:
             scatter_on_scalar(m_new[2], m_val[:, 2, :], part)
         for planes, tables, j in ((o0_planes, w_new, 0), (o1_planes, m_new, 0), (o0_planes, w_new, 2), (o0_planes, w_new, 1), (o0_planes, w_new, 3), (o1_planes, m_new, 1), (o1_planes, m_new, 3)):

@@ -141,47 +141,49 @@ def tile_attend_gsq_pl_nag_kernel(tc, xT, wT, y, wt, xm, mT, offs, out_0, out_1,
         flat = keep.tile([P, L * T], BF16, name="rounded")
         rounded = flat[:].rearrange("p (j t) -> p j t", j=L)
         m_val = keep.tile([P, L, N], F32, name="m_val")
-        steps = [keep.tile([P, N], F32, name=f"m_step{j}", tag=f"m_step{j}")[:] for j in range(L - 1)] + [m_val[:, 2, :]]
-        m_step = [[step[:, part] for part in halves] for step in steps]
-        ahead = [keep.tile([P, N], F32, name=f"ahead{j}", tag=f"ahead{j}") for j in range(L - 1)]
+        steps = [keep.tile([P, N], F32, name=f"m_step{j}")[:] for j in range(L - 1)] + [m_val[:, 2, :]]
+        sums = [keep.tile([P, N], F32, name=f"sum{j}")[:] for j in range(L - 1)] + [flat[:, T : T + 2 * N].bitcast(F32)]
         m_new = [keep.tile([P, T], F32, name=f"m_new{j}", tag=f"table{j}") for j in range(L)]
-        for j in (3, 2):
+        for j in (2, 3):
             nc.sync.dma_start(m_new[j][:], m_planes[:, j, :])
 
         def scatter_on_scalar(window, values, part):
             nc.scalar.activation(listed(window, part), values[:, part], COPY)
 
-        def momentum(j, part, step):
-            nc.vector.scalar_tensor_tensor(m_val[:, j, part], step, BETA / MOM_STEP, grad[j][:, part], MULT, ADD)
+        def momentum(j, part):
+            nc.vector.scalar_tensor_tensor(m_val[:, j, part], steps[j][:, part], BETA / MOM_STEP, grad[j][:, part], MULT, ADD)
 
         for j in range(L):
-            if j > 0:
-                nc.vector.tensor_scalar(steps[j][:], listed(m_src[j], whole[0]), MOM_STEP, 0.0, MULT, ADD)
             if j == 0:
-                nc.scalar.activation(steps[j][:], listed(m_src[j], whole[0]), COPY, scale=MOM_STEP)
+                nc.scalar.activation(steps[j], listed(m_src[j], whole[0]), COPY, scale=MOM_STEP)
                 nc.scalar.activation(m_new[j][:], m_src[j][:], COPY)
+            else:
+                nc.vector.tensor_scalar(steps[j], listed(m_src[j], whole[0]), MOM_STEP, 0.0, MULT, ADD)
             if j == 1:
                 nc.vector.tensor_copy(m_new[j][:], m_src[j][:])
-            if j != 2:
-                sums = [flat[:, T : T + N].bitcast(F32), m_val[:, 1, halves[1]]] if j == L - 1 else [ahead[j][:, part] for part in halves]
-                for part, total, step in zip(halves, sums, m_step[j]):
-                    nc.vector.tensor_tensor(total, w_got[:, j, part], step, ADD)
-                for h, part in enumerate(halves):
-                    nc.vector.scalar_tensor_tensor(w_got[:, j, part], grad[j][:, part], GRAD_STEP, sums[h], MULT, ADD)
+            on_vector = (None, None, whole[0], halves[0])[j]
+            on_scalar = (whole[0], whole[0], None, halves[1])[j]
+            if on_vector:
+                nc.vector.scalar_tensor_tensor(sums[j][:, on_vector], grad[j][:, on_vector], GRAD_STEP, steps[j][:, on_vector], MULT, ADD)
+            if on_scalar:
+                nc.vector.tensor_tensor(sums[j][:, on_scalar], w_got[:, j, on_scalar], steps[j][:, on_scalar], ADD)
+            if j < 2:
+                for part in halves:
+                    momentum(j, part)
+                    nc.vector.scalar_tensor_tensor(w_got[:, j, part], grad[j][:, part], GRAD_STEP, sums[j][:, part], MULT, ADD)
                     scatter_on_scalar(w_new[j], w_got[:, j, :], part)
-                    if (j, h) == (L - 1, 1):
-                        momentum(1, part, m_step[1][h])
-                        nc.vector.tensor_copy(listed(m_new[1], part), m_val[:, 1, part])
-                    if (j, h) != (1, 1):
-                        momentum(j, part, m_step[j][h])
-                        scatter_on_scalar(m_new[j], m_val[:, j, :], part)
-            else:
-                nc.vector.scalar_tensor_tensor(ahead[j][:], grad[j][:], GRAD_STEP, steps[j][:], MULT, ADD)
-                nc.vector.tensor_tensor(listed(w_new[j], whole[0]), ahead[j][:], w_got[:, j, :], ADD)
-        momentum(2, whole[0], steps[2][:])
+                    scatter_on_scalar(m_new[j], m_val[:, j, :], part)
+            if j == 3:
+                nc.vector.scalar_tensor_tensor(w_got[:, j, on_scalar], grad[j][:, on_scalar], GRAD_STEP, sums[j][:, on_scalar], MULT, ADD)
+            if on_vector:
+                nc.vector.tensor_tensor(listed(w_new[j], on_vector), sums[j][:, on_vector], w_got[:, j, on_vector], ADD)
+        scatter_on_scalar(w_new[3], w_got[:, 3, :], halves[1])
+        momentum(3, whole[0])
+        momentum(2, whole[0])
         for part in halves:
-            scatter_on_scalar(m_new[2], m_val[:, 2, :], part)
-        for planes, tables, j in ((o0_planes, w_new, 0), (o1_planes, m_new, 0), (o0_planes, w_new, 2), (o0_planes, w_new, 1), (o0_planes, w_new, 3), (o1_planes, m_new, 1), (o1_planes, m_new, 3)):
+            for j in (2, 3):
+                scatter_on_scalar(m_new[j], m_val[:, j, :], part)
+        for planes, tables, j in ((o0_planes, w_new, 0), (o1_planes, m_new, 0), (o0_planes, w_new, 2), (o0_planes, w_new, 1), (o1_planes, m_new, 1), (o0_planes, w_new, 3), (o1_planes, m_new, 2)):
             nc.sync.dma_start(planes[:, j, :], tables[j][:])
 
         for j in (0, 2):
@@ -202,6 +204,6 @@ def tile_attend_gsq_pl_nag_kernel(tc, xT, wT, y, wt, xm, mT, offs, out_0, out_1,
                 done = slice(0, cols.stop) if q == 1 else cols
                 nc.sync.dma_start(words_out[:, done], out_codes[q - 1][:].bitcast(I32))
             if q == 1:
-                nc.sync.dma_start(o1_planes[:, 2, :], m_new[2][:])
+                nc.sync.dma_start(o1_planes[:, 3, :], m_new[3][:])
         for f in range(4):
             nc.sync.dma_start(scales_out[4 * f : 4 * f + 4, :].rearrange("i (q c) -> q i c", q=4), out_scales[32 * f : 32 * f + 16, :].bitcast(I32))

@@ -141,8 +141,13 @@ def tile_attend_gsq_pl_nag_kernel(tc, xT, wT, y, wt, xm, mT, offs, out_0, out_1,
         flat = keep.tile([P, L * T], BF16, name="rounded")
         rounded = flat[:].rearrange("p (j t) -> p j t", j=L)
         m_val = keep.tile([P, L, N], F32, name="m_val")
-        steps = [keep.tile([P, N], F32, name=f"m_step{j}")[:] for j in range(L - 1)] + [m_val[:, 2, :]]
-        sums = [keep.tile([P, N], F32, name=f"sum{j}")[:] for j in range(L - 1)] + [flat[:, T : T + 2 * N].bitcast(F32)]
+
+        def borrowed(plane, start, count):
+            return rounded[:, plane, start : start + 2 * count].bitcast(F32)
+
+        steps = [keep.tile([P, N], F32, name="step0")[:], borrowed(2, T // 4, N), keep.tile([P, N], F32, name="step2")[:], m_val[:, 2, :]]
+        sums = [keep.tile([P, N], F32, name="sum0")[:], borrowed(0, T // 2, N), None, borrowed(1, 0, N)]
+        descended = [None, None, sums[1], borrowed(2, T // 2, N // 2)]
         m_new = [keep.tile([P, T], F32, name=f"m_new{j}", tag=f"table{j}") for j in range(L)]
         for j in (2, 3):
             nc.sync.dma_start(m_new[j][:], m_planes[:, j, :])
@@ -163,8 +168,6 @@ def tile_attend_gsq_pl_nag_kernel(tc, xT, wT, y, wt, xm, mT, offs, out_0, out_1,
                 nc.vector.tensor_copy(m_new[j][:], m_src[j][:])
             on_vector = (None, None, whole[0], halves[0])[j]
             on_scalar = (whole[0], whole[0], None, halves[1])[j]
-            if on_vector:
-                nc.vector.scalar_tensor_tensor(sums[j][:, on_vector], grad[j][:, on_vector], GRAD_STEP, steps[j][:, on_vector], MULT, ADD)
             if on_scalar:
                 nc.vector.tensor_tensor(sums[j][:, on_scalar], w_got[:, j, on_scalar], steps[j][:, on_scalar], ADD)
             if j < 2:
@@ -176,7 +179,10 @@ def tile_attend_gsq_pl_nag_kernel(tc, xT, wT, y, wt, xm, mT, offs, out_0, out_1,
             if j == 3:
                 nc.vector.scalar_tensor_tensor(w_got[:, j, on_scalar], grad[j][:, on_scalar], GRAD_STEP, sums[j][:, on_scalar], MULT, ADD)
             if on_vector:
-                nc.vector.tensor_tensor(listed(w_new[j], on_vector), sums[j][:, on_vector], w_got[:, j, on_vector], ADD)
+                nc.vector.tensor_tensor(listed(w_new[j], on_vector), descended[j][:, on_vector], steps[j][:, on_vector], ADD)
+            if j == 1:
+                for k, part in ((2, whole[0]), (3, halves[0])):
+                    nc.vector.scalar_tensor_tensor(descended[k][:, part], grad[k][:, part], GRAD_STEP, w_got[:, k, part], MULT, ADD)
         scatter_on_scalar(w_new[3], w_got[:, 3, :], halves[1])
         momentum(3, whole[0])
         momentum(2, whole[0])
@@ -186,11 +192,12 @@ def tile_attend_gsq_pl_nag_kernel(tc, xT, wT, y, wt, xm, mT, offs, out_0, out_1,
         for planes, tables, j in ((o0_planes, w_new, 0), (o1_planes, m_new, 0), (o0_planes, w_new, 2), (o0_planes, w_new, 1), (o1_planes, m_new, 1), (o0_planes, w_new, 3), (o1_planes, m_new, 2)):
             nc.sync.dma_start(planes[:, j, :], tables[j][:])
 
-        for j in (0, 2):
-            for part in (slice(0, T // 2), slice(T // 2, T)):
-                nc.gpsimd.tensor_copy(rounded[:, j, part], w_new[j][:, part])
-        for j in (1, 3):
-            nc.vector.tensor_copy(rounded[:, j, :], w_new[j][:])
+        share = slice(0, 5 * T // 8)
+        rest = slice(5 * T // 8, T)
+        for j, part in ((0, slice(0, T // 2)), (0, slice(T // 2, T)), (2, share)):
+            nc.gpsimd.tensor_copy(rounded[:, j, part], w_new[j][:, part])
+        for j, part in ((2, rest), (1, slice(0, T)), (3, slice(0, T))):
+            nc.vector.tensor_copy(rounded[:, j, part], w_new[j][:, part])
         quarter = T // 4
         out_scales = keep.tile([P, quarter], U8, name="out_scales", align_bytes=64)
         out_codes = [keep.tile([P, width], U32, name=f"out_codes{k}", align_bytes=64) for k, width in enumerate((2 * quarter, quarter, quarter))]

@@ -149,8 +149,8 @@ def tile_attend_gsq_pl_nag_kernel(tc, xT, wT, y, wt, xm, mT, offs, out_0, out_1,
         sums = [keep.tile([P, N], F32, name="sum0")[:], borrowed(0, T // 2, N), None, borrowed(1, 0, N)]
         descended = [None, None, sums[1], borrowed(2, T // 2, N // 2)]
         m_new = [keep.tile([P, T], F32, name=f"m_new{j}", tag=f"table{j}") for j in range(L)]
-        for j in (2, 3):
-            nc.sync.dma_start(m_new[j][:], m_planes[:, j, :])
+        nc.sync.dma_start(m_new[2][:], m_planes[:, 2, :])
+        nc.sync.dma_start(m_new[3][:, : T // 2], m_planes[:, 3, : T // 2])
 
         def scatter_on_scalar(window, values, part):
             nc.scalar.activation(listed(window, part), values[:, part], COPY)
@@ -161,11 +161,14 @@ def tile_attend_gsq_pl_nag_kernel(tc, xT, wT, y, wt, xm, mT, offs, out_0, out_1,
         for j in range(L):
             if j == 0:
                 nc.scalar.activation(steps[j], listed(m_src[j], whole[0]), COPY, scale=MOM_STEP)
-                nc.scalar.activation(m_new[j][:], m_src[j][:], COPY)
+                nc.scalar.activation(m_new[j][:, : T // 2], m_src[j][:, : T // 2], COPY)
+                nc.vector.tensor_copy(m_new[j][:, T // 2 :], m_src[j][:, T // 2 :])
             else:
                 nc.vector.tensor_scalar(steps[j], listed(m_src[j], whole[0]), MOM_STEP, 0.0, MULT, ADD)
             if j == 1:
                 nc.vector.tensor_copy(m_new[j][:], m_src[j][:])
+            if j == 3:
+                nc.scalar.activation(m_new[j][:, T // 2 :], m_src[j][:, T // 2 :], COPY)
             on_vector = (None, None, whole[0], halves[0])[j]
             on_scalar = (whole[0], whole[0], None, halves[1])[j]
             if on_scalar:

@@ -141,16 +141,14 @@ def tile_attend_gsq_pl_nag_kernel(tc, xT, wT, y, wt, xm, mT, offs, out_0, out_1,
         flat = keep.tile([P, L * T], BF16, name="rounded")
         rounded = flat[:].rearrange("p (j t) -> p j t", j=L)
         m_val = keep.tile([P, L, N], F32, name="m_val")
-
-        def borrowed(plane, start, count):
-            return rounded[:, plane, start : start + 2 * count].bitcast(F32)
-
-        steps = [keep.tile([P, N], F32, name="step0")[:], borrowed(2, T // 4, N), keep.tile([P, N], F32, name="step2")[:], m_val[:, 2, :]]
-        sums = [keep.tile([P, N], F32, name="sum0")[:], borrowed(0, T // 2, N), None, borrowed(1, 0, N)]
-        descended = [None, None, sums[1], borrowed(2, T // 2, N // 2)]
+        steps = [keep.tile([P, N], F32, name=f"step{j}")[:] for j in range(L - 1)] + [m_val[:, 2, :]]
+        sums = [keep.tile([P, N], F32, name=f"sum{j}")[:] for j in range(2)] + [None, flat[:, T : T + 2 * N].bitcast(F32)]
+        descended = [None, None, sums[1], steps[1]]
         m_new = [keep.tile([P, T], F32, name=f"m_new{j}", tag=f"table{j}") for j in range(L)]
+        loaded = slice(0, 5 * T // 8)
+        copied = slice(5 * T // 8, T)
+        nc.sync.dma_start(m_new[3][:, loaded], m_planes[:, 3, loaded])
         nc.sync.dma_start(m_new[2][:], m_planes[:, 2, :])
-        nc.sync.dma_start(m_new[3][:, : T // 2], m_planes[:, 3, : T // 2])
 
         def scatter_on_scalar(window, values, part):
             nc.scalar.activation(listed(window, part), values[:, part], COPY)
@@ -168,7 +166,7 @@ def tile_attend_gsq_pl_nag_kernel(tc, xT, wT, y, wt, xm, mT, offs, out_0, out_1,
             if j == 1:
                 nc.vector.tensor_copy(m_new[j][:], m_src[j][:])
             if j == 3:
-                nc.scalar.activation(m_new[j][:, T // 2 :], m_src[j][:, T // 2 :], COPY)
+                nc.scalar.activation(m_new[j][:, copied], m_src[j][:, copied], COPY)
             on_vector = (None, None, whole[0], halves[0])[j]
             on_scalar = (whole[0], whole[0], None, halves[1])[j]
             if on_scalar:
@@ -189,18 +187,17 @@ def tile_attend_gsq_pl_nag_kernel(tc, xT, wT, y, wt, xm, mT, offs, out_0, out_1,
         scatter_on_scalar(w_new[3], w_got[:, 3, :], halves[1])
         momentum(3, whole[0])
         momentum(2, whole[0])
-        for part in halves:
-            for j in (2, 3):
+        for j in (3, 2):
+            for part in halves:
                 scatter_on_scalar(m_new[j], m_val[:, j, :], part)
-        for planes, tables, j in ((o0_planes, w_new, 0), (o1_planes, m_new, 0), (o0_planes, w_new, 2), (o0_planes, w_new, 1), (o1_planes, m_new, 1), (o0_planes, w_new, 3), (o1_planes, m_new, 2)):
+        for planes, tables, j in ((o0_planes, w_new, 0), (o1_planes, m_new, 0), (o0_planes, w_new, 2), (o0_planes, w_new, 1), (o1_planes, m_new, 1), (o0_planes, w_new, 3), (o1_planes, m_new, 3)):
             nc.sync.dma_start(planes[:, j, :], tables[j][:])
 
-        share = slice(0, 5 * T // 8)
-        rest = slice(5 * T // 8, T)
-        for j, part in ((0, slice(0, T // 2)), (0, slice(T // 2, T)), (2, share)):
-            nc.gpsimd.tensor_copy(rounded[:, j, part], w_new[j][:, part])
-        for j, part in ((2, rest), (1, slice(0, T)), (3, slice(0, T))):
-            nc.vector.tensor_copy(rounded[:, j, part], w_new[j][:, part])
+        for j in (0, 2):
+            for part in (slice(0, T // 2), slice(T // 2, T)):
+                nc.gpsimd.tensor_copy(rounded[:, j, part], w_new[j][:, part])
+        for j in (1, 3):
+            nc.vector.tensor_copy(rounded[:, j, :], w_new[j][:])
         quarter = T // 4
         out_scales = keep.tile([P, quarter], U8, name="out_scales", align_bytes=64)
         out_codes = [keep.tile([P, width], U32, name=f"out_codes{k}", align_bytes=64) for k, width in enumerate((2 * quarter, quarter, quarter))]
@@ -214,6 +211,6 @@ def tile_attend_gsq_pl_nag_kernel(tc, xT, wT, y, wt, xm, mT, offs, out_0, out_1,
                 done = slice(0, cols.stop) if q == 1 else cols
                 nc.sync.dma_start(words_out[:, done], out_codes[q - 1][:].bitcast(I32))
             if q == 1:
-                nc.sync.dma_start(o1_planes[:, 3, :], m_new[3][:])
+                nc.sync.dma_start(o1_planes[:, 2, :], m_new[2][:])
         for f in range(4):
             nc.sync.dma_start(scales_out[4 * f : 4 * f + 4, :].rearrange("i (q c) -> q i c", q=4), out_scales[32 * f : 32 * f + 16, :].bitcast(I32))

@@ -196,8 +196,8 @@ def tile_attend_gsq_pl_nag_kernel(tc, xT, wT, y, wt, xm, mT, offs, out_0, out_1,
         for j in (0, 2):
             for part in (slice(0, T // 2), slice(T // 2, T)):
                 nc.gpsimd.tensor_copy(rounded[:, j, part], w_new[j][:, part])
-        for j in (1, 3):
-            nc.vector.tensor_copy(rounded[:, j, :], w_new[j][:])
+        for j, part in ((1, slice(0, T)), (3, slice(0, T // 4)), (3, slice(T // 4, T))):
+            nc.vector.tensor_copy(rounded[:, j, part], w_new[j][:, part])
         quarter = T // 4
         out_scales = keep.tile([P, quarter], U8, name="out_scales", align_bytes=64)
         out_codes = [keep.tile([P, width], U32, name=f"out_codes{k}", align_bytes=64) for k, width in enumerate((2 * quarter, quarter, quarter))]

@@ -141,8 +141,8 @@ def tile_attend_gsq_pl_nag_kernel(tc, xT, wT, y, wt, xm, mT, offs, out_0, out_1,
         flat = keep.tile([P, L * T], BF16, name="rounded")
         rounded = flat[:].rearrange("p (j t) -> p j t", j=L)
         m_val = keep.tile([P, L, N], F32, name="m_val")
-        steps = [keep.tile([P, N], F32, name=f"step{j}")[:] for j in range(L - 1)] + [m_val[:, 2, :]]
-        sums = [keep.tile([P, N], F32, name=f"sum{j}")[:] for j in range(2)] + [None, flat[:, T : T + 2 * N].bitcast(F32)]
+        steps = [keep.tile([P, N], F32, name="step0")[:], flat[:, 2 * T + 2 * N : 2 * T + 4 * N].bitcast(F32), keep.tile([P, N], F32, name="step2")[:], m_val[:, 2, :]]
+        sums = [keep.tile([P, N], F32, name="sum0")[:], keep.tile([P, N], F32, name="sum1")[:], None, flat[:, T : T + 2 * N].bitcast(F32)]
         descended = [None, None, sums[1], steps[1]]
         m_new = [keep.tile([P, T], F32, name=f"m_new{j}", tag=f"table{j}") for j in range(L)]
         loaded = slice(0, 5 * T // 8)
@@ -171,7 +171,15 @@ def tile_attend_gsq_pl_nag_kernel(tc, xT, wT, y, wt, xm, mT, offs, out_0, out_1,
             on_scalar = (whole[0], whole[0], None, halves[1])[j]
             if on_scalar:
                 nc.vector.tensor_tensor(sums[j][:, on_scalar], w_got[:, j, on_scalar], steps[j][:, on_scalar], ADD)
-            if j < 2:
+            if j == 0:
+                momentum(j, halves[0])
+                scatter_on_scalar(m_new[j], m_val[:, j, :], halves[0])
+                for part in halves:
+                    nc.vector.scalar_tensor_tensor(w_got[:, j, part], grad[j][:, part], GRAD_STEP, sums[j][:, part], MULT, ADD)
+                    scatter_on_scalar(w_new[j], w_got[:, j, :], part)
+                nc.vector.scalar_tensor_tensor(sums[j][:, halves[0]], steps[j][:, halves[1]], BETA / MOM_STEP, grad[j][:, halves[1]], MULT, ADD)
+                nc.scalar.activation(listed(m_new[j], halves[1]), sums[j][:, halves[0]], COPY)
+            if j == 1:
                 for part in halves:
                     momentum(j, part)
                     nc.vector.scalar_tensor_tensor(w_got[:, j, part], grad[j][:, part], GRAD_STEP, sums[j][:, part], MULT, ADD)
@@ -190,12 +198,12 @@ def tile_attend_gsq_pl_nag_kernel(tc, xT, wT, y, wt, xm, mT, offs, out_0, out_1,
         for j in (3, 2):
             for part in halves:
                 scatter_on_scalar(m_new[j], m_val[:, j, :], part)
-        for planes, tables, j in ((o0_planes, w_new, 0), (o1_planes, m_new, 0), (o0_planes, w_new, 2), (o0_planes, w_new, 1), (o1_planes, m_new, 1), (o0_planes, w_new, 3), (o1_planes, m_new, 3)):
+        for planes, tables, j in ((o0_planes, w_new, 0), (o1_planes, m_new, 0), (o0_planes, w_new, 2), (o1_planes, m_new, 1), (o0_planes, w_new, 1), (o0_planes, w_new, 3), (o1_planes, m_new, 3)):
             nc.sync.dma_start(planes[:, j, :], tables[j][:])
 
-        for j in (0, 2):
-            for part in (slice(0, T // 2), slice(T // 2, T)):
-                nc.gpsimd.tensor_copy(rounded[:, j, part], w_new[j][:, part])
+        for j, start, stop in ((0, 0, 1), (0, 1, 4), (0, 4, 8), (2, 0, 4), (2, 4, 8)):
+            part = slice(start * T // 8, stop * T // 8)
+            nc.gpsimd.tensor_copy(rounded[:, j, part], w_new[j][:, part])
         for j, part in ((1, slice(0, T)), (3, slice(0, T // 4)), (3, slice(T // 4, T))):
             nc.vector.tensor_copy(rounded[:, j, part], w_new[j][:, part])
         quarter = T // 4

@@ -148,7 +148,7 @@ def tile_attend_gsq_pl_nag_kernel(tc, xT, wT, y, wt, xm, mT, offs, out_0, out_1,
         loaded = slice(0, 5 * T // 8)
         copied = slice(5 * T // 8, T)
         nc.sync.dma_start(m_new[3][:, loaded], m_planes[:, 3, loaded])
-        nc.sync.dma_start(m_new[2][:], m_planes[:, 2, :])
+        nc.sync.dma_start(m_new[2][:, loaded], m_planes[:, 2, loaded])
 
         def scatter_on_scalar(window, values, part):
             nc.scalar.activation(listed(window, part), values[:, part], COPY)
@@ -165,6 +165,8 @@ def tile_attend_gsq_pl_nag_kernel(tc, xT, wT, y, wt, xm, mT, offs, out_0, out_1,
                 nc.vector.tensor_scalar(steps[j], listed(m_src[j], whole[0]), MOM_STEP, 0.0, MULT, ADD)
             if j == 1:
                 nc.vector.tensor_copy(m_new[j][:], m_src[j][:])
+            if j == 2:
+                nc.vector.tensor_copy(m_new[j][:, copied], m_src[j][:, copied])
             if j == 3:
                 nc.scalar.activation(m_new[j][:, copied], m_src[j][:, copied], COPY)
             on_vector = (None, None, whole[0], halves[0])[j]

@@ -83,7 +83,7 @@ def tile_attend_gsq_pl_nag_kernel(tc, xT, wT, y, wt, xm, mT, offs, out_0, out_1,
         nc.sync.dma_start(xm_raw[:], xm_rows)
         m_src = [keep.tile([P, T], F32, name=f"m_src{j}") for j in range(L)]
         w_new = [keep.tile([P, T], F32, name=f"w_new{j}") for j in range(L - 1)]
-        for j in range(L):
+        for j in range(L - 1):
             nc.sync.dma_start(m_src[j][:], m_planes[:, j, :])
 
         w_got = keep.tile([P, L, N], F32, name="w_got")
@@ -138,89 +138,88 @@ def tile_attend_gsq_pl_nag_kernel(tc, xT, wT, y, wt, xm, mT, offs, out_0, out_1,
         deal(xm_bf, xm_raw, slice(2, 4), nc.vector.tensor_copy)
         gradient_pair(1)
 
+        first, second = halves
         flat = keep.tile([P, L * T], BF16, name="rounded")
         rounded = flat[:].rearrange("p (j t) -> p j t", j=L)
         m_val = keep.tile([P, L, N], F32, name="m_val")
-        steps = [keep.tile([P, N], F32, name="step0")[:], flat[:, 2 * T + 2 * N : 2 * T + 4 * N].bitcast(F32), keep.tile([P, N], F32, name="step2")[:], m_val[:, 2, :]]
-        sums = [keep.tile([P, N], F32, name="sum0")[:], keep.tile([P, N], F32, name="sum1")[:], None, flat[:, T : T + 2 * N].bitcast(F32)]
-        descended = [None, None, sums[1], steps[1]]
+        steps = [flat[:, T + N : T + 3 * N].bitcast(F32) if j == 2 else keep.tile([P, N], F32, name=f"step{j}")[:] for j in range(L)]
+        sums = [keep.tile([P, N], F32, name=f"sum{j}")[:] for j in range(2)]
         m_new = [keep.tile([P, T], F32, name=f"m_new{j}", tag=f"table{j}") for j in range(L)]
         loaded = slice(0, 5 * T // 8)
         copied = slice(5 * T // 8, T)
+        nc.sync.dma_start(m_new[2][:], m_planes[:, 2, :])
+        nc.sync.dma_start(m_src[3][:], m_planes[:, 3, :])
         nc.sync.dma_start(m_new[3][:, loaded], m_planes[:, 3, loaded])
-        nc.sync.dma_start(m_new[2][:, loaded], m_planes[:, 2, loaded])
 
         def scatter_on_scalar(window, values, part):
-            nc.scalar.activation(listed(window, part), values[:, part], COPY)
+            nc.scalar.activation(listed(window, part), values, COPY)
 
-        def momentum(j, part):
-            nc.vector.scalar_tensor_tensor(m_val[:, j, part], steps[j][:, part], BETA / MOM_STEP, grad[j][:, part], MULT, ADD)
+        def gather(j):
+            nc.vector.tensor_scalar(steps[j], listed(m_src[j], whole[0]), MOM_STEP, 0.0, MULT, ADD)
 
-        for j in range(L):
-            if j == 0:
-                nc.scalar.activation(steps[j], listed(m_src[j], whole[0]), COPY, scale=MOM_STEP)
-                nc.scalar.activation(m_new[j][:, : T // 2], m_src[j][:, : T // 2], COPY)
-                nc.vector.tensor_copy(m_new[j][:, T // 2 :], m_src[j][:, T // 2 :])
-            else:
-                nc.vector.tensor_scalar(steps[j], listed(m_src[j], whole[0]), MOM_STEP, 0.0, MULT, ADD)
-            if j == 1:
-                nc.vector.tensor_copy(m_new[j][:], m_src[j][:])
-            if j == 2:
-                nc.vector.tensor_copy(m_new[j][:, copied], m_src[j][:, copied])
-            if j == 3:
-                nc.scalar.activation(m_new[j][:, copied], m_src[j][:, copied], COPY)
-            on_vector = (None, None, whole[0], halves[0])[j]
-            on_scalar = (whole[0], whole[0], None, halves[1])[j]
-            if on_scalar:
-                nc.vector.tensor_tensor(sums[j][:, on_scalar], w_got[:, j, on_scalar], steps[j][:, on_scalar], ADD)
-            if j == 0:
-                momentum(j, halves[0])
-                scatter_on_scalar(m_new[j], m_val[:, j, :], halves[0])
-                for part in halves:
-                    nc.vector.scalar_tensor_tensor(w_got[:, j, part], grad[j][:, part], GRAD_STEP, sums[j][:, part], MULT, ADD)
-                    scatter_on_scalar(w_new[j], w_got[:, j, :], part)
-                nc.vector.scalar_tensor_tensor(sums[j][:, halves[0]], steps[j][:, halves[1]], BETA / MOM_STEP, grad[j][:, halves[1]], MULT, ADD)
-                nc.scalar.activation(listed(m_new[j], halves[1]), sums[j][:, halves[0]], COPY)
-            if j == 1:
-                for part in halves:
-                    momentum(j, part)
-                    nc.vector.scalar_tensor_tensor(w_got[:, j, part], grad[j][:, part], GRAD_STEP, sums[j][:, part], MULT, ADD)
-                    scatter_on_scalar(w_new[j], w_got[:, j, :], part)
-                    scatter_on_scalar(m_new[j], m_val[:, j, :], part)
-            if j == 3:
-                nc.vector.scalar_tensor_tensor(w_got[:, j, on_scalar], grad[j][:, on_scalar], GRAD_STEP, sums[j][:, on_scalar], MULT, ADD)
-            if on_vector:
-                nc.vector.tensor_tensor(listed(w_new[j], on_vector), descended[j][:, on_vector], steps[j][:, on_vector], ADD)
-            if j == 1:
-                for k, part in ((2, whole[0]), (3, halves[0])):
-                    nc.vector.scalar_tensor_tensor(descended[k][:, part], grad[k][:, part], GRAD_STEP, w_got[:, k, part], MULT, ADD)
-        scatter_on_scalar(w_new[3], w_got[:, 3, :], halves[1])
-        momentum(3, whole[0])
-        momentum(2, whole[0])
-        for j in (3, 2):
-            for part in halves:
-                scatter_on_scalar(m_new[j], m_val[:, j, :], part)
-        for planes, tables, j in ((o0_planes, w_new, 0), (o1_planes, m_new, 0), (o0_planes, w_new, 2), (o1_planes, m_new, 1), (o0_planes, w_new, 1), (o0_planes, w_new, 3), (o1_planes, m_new, 3)):
+        def momentum(dst, j, part):
+            nc.vector.scalar_tensor_tensor(dst, steps[j][:, part], BETA / MOM_STEP, grad[j][:, part], MULT, ADD)
+
+        def descend(dst, j, part, src):
+            nc.vector.scalar_tensor_tensor(dst, grad[j][:, part], GRAD_STEP, src, MULT, ADD)
+
+        nc.scalar.activation(steps[0], listed(m_src[0], whole[0]), COPY, scale=MOM_STEP)
+        nc.scalar.activation(m_new[0][:, : T // 2], m_src[0][:, : T // 2], COPY)
+        nc.vector.tensor_copy(m_new[0][:, T // 2 :], m_src[0][:, T // 2 :])
+        nc.vector.tensor_tensor(sums[0], w_got[:, 0, :], steps[0], ADD)
+        momentum(m_val[:, 0, first], 0, first)
+        scatter_on_scalar(m_new[0], m_val[:, 0, first], first)
+        for part in halves:
+            descend(w_got[:, 0, part], 0, part, sums[0][:, part])
+            scatter_on_scalar(w_new[0], w_got[:, 0, part], part)
+        momentum(sums[0][:, first], 0, second)
+        scatter_on_scalar(m_new[0], sums[0][:, first], second)
+        gather(1)
+        nc.vector.tensor_copy(m_new[1][:], m_src[1][:])
+        nc.vector.tensor_tensor(sums[1], w_got[:, 1, :], steps[1], ADD)
+        momentum(m_val[:, 1, first], 1, first)
+        scatter_on_scalar(m_new[1], m_val[:, 1, first], first)
+        descend(sums[0][:, second], 1, first, sums[1][:, first])
+        scatter_on_scalar(w_new[1], sums[0][:, second], first)
+        momentum(m_val[:, 1, second], 1, second)
+        scatter_on_scalar(m_new[1], m_val[:, 1, second], second)
+        descend(w_got[:, 1, :], 2, whole[0], w_got[:, 2, :])
+        gather(2)
+        nc.vector.tensor_tensor(listed(w_new[2], whole[0]), w_got[:, 1, :], steps[2], ADD)
+        momentum(m_val[:, 2, first], 2, first)
+        descend(w_got[:, 1, second], 1, second, sums[1][:, second])
+        scatter_on_scalar(w_new[1], w_got[:, 1, second], second)
+        descend(sums[1], 3, whole[0], w_got[:, 3, :])
+        scatter_on_scalar(m_new[2], m_val[:, 2, first], first)
+        for part in halves:
+            nc.vector.tensor_copy(steps[3][:, part], listed(m_src[3], part))
+        nc.scalar.activation(m_new[3][:, copied], m_src[3][:, copied], COPY)
+        for part in halves:
+            nc.vector.scalar_tensor_tensor(w_got[:, 3, part], steps[3][:, part], MOM_STEP, sums[1][:, part], MULT, ADD)
+        momentum(sums[1][:, first], 2, second)
+        nc.vector.tensor_copy(listed(w_new[3], whole[0]), w_got[:, 3, :])
+        nc.vector.scalar_tensor_tensor(w_got[:, 3, :], steps[3], BETA, grad[3][:], MULT, ADD)
+        nc.scalar.activation(rounded[:, 3, T // 2 :], w_new[3][:, T // 2 :], COPY)
+        scatter_on_scalar(m_new[2], sums[1][:, first], second)
+        for part in halves:
+            scatter_on_scalar(m_new[3], w_got[:, 3, part], part)
+        for planes, tables, j in ((o1_planes, m_new, 0), (o0_planes, w_new, 0), (o0_planes, w_new, 2), (o1_planes, m_new, 1), (o0_planes, w_new, 1), (o0_planes, w_new, 3), (o1_planes, m_new, 2)):
             nc.sync.dma_start(planes[:, j, :], tables[j][:])
 
-        for j, start, stop in ((0, 0, 1), (0, 1, 4), (0, 4, 8), (2, 0, 4), (2, 4, 8)):
+        for j, start, stop in ((0, 0, 1), (0, 1, 4), (0, 4, 8), (2, 0, 4), (2, 4, 8), (1, 0, 4), (1, 4, 8), (3, 0, 2)):
             part = slice(start * T // 8, stop * T // 8)
             nc.gpsimd.tensor_copy(rounded[:, j, part], w_new[j][:, part])
-        for j, part in ((1, slice(0, T)), (3, slice(0, T // 4)), (3, slice(T // 4, T))):
-            nc.vector.tensor_copy(rounded[:, j, part], w_new[j][:, part])
+        nc.vector.tensor_copy(rounded[:, 3, T // 4 : T // 2], w_new[3][:, T // 4 : T // 2])
         quarter = T // 4
         out_scales = keep.tile([P, quarter], U8, name="out_scales", align_bytes=64)
-        out_codes = [keep.tile([P, width], U32, name=f"out_codes{k}", align_bytes=64) for k, width in enumerate((2 * quarter, quarter, quarter))]
-        code_cols = [out_codes[0][:, :quarter], out_codes[0][:, quarter:], out_codes[1][:], out_codes[2][:]]
+        out_codes = [keep.tile([P, width], U32, name=f"out_codes{k}", align_bytes=64) for k, width in enumerate((quarter,) * 4)]
         for q in range(4):
             cols = slice(q * quarter, (q + 1) * quarter)
             out_bf = keep.tile([P, L * quarter], BF16, name=f"out_bf{q}", align_bytes=64)
             weave(out_bf[:], rounded[:, :, cols])
-            nc.vector.quantize_mx(out=code_cols[q].bitcast(E4M3), scales=out_scales[4 * q :, :], in_=out_bf[:])
-            if q > 0:
-                done = slice(0, cols.stop) if q == 1 else cols
-                nc.sync.dma_start(words_out[:, done], out_codes[q - 1][:].bitcast(I32))
+            nc.vector.quantize_mx(out=out_codes[q][:].bitcast(E4M3), scales=out_scales[4 * q :, :], in_=out_bf[:])
+            nc.sync.dma_start(words_out[:, cols], out_codes[q][:].bitcast(I32))
             if q == 1:
-                nc.sync.dma_start(o1_planes[:, 2, :], m_new[2][:])
+                nc.sync.dma_start(o1_planes[:, 3, :], m_new[3][:])
         for f in range(4):
             nc.sync.dma_start(scales_out[4 * f : 4 * f + 4, :].rearrange("i (q c) -> q i c", q=4), out_scales[32 * f : 32 * f + 16, :].bitcast(I32))

@@ -145,11 +145,11 @@ def tile_attend_gsq_pl_nag_kernel(tc, xT, wT, y, wt, xm, mT, offs, out_0, out_1,
         steps = [flat[:, T + N : T + 3 * N].bitcast(F32) if j == 2 else keep.tile([P, N], F32, name=f"step{j}")[:] for j in range(L)]
         sums = [keep.tile([P, N], F32, name=f"sum{j}")[:] for j in range(2)]
         m_new = [keep.tile([P, T], F32, name=f"m_new{j}", tag=f"table{j}") for j in range(L)]
-        loaded = slice(0, 5 * T // 8)
-        copied = slice(5 * T // 8, T)
-        nc.sync.dma_start(m_new[2][:], m_planes[:, 2, :])
+        loaded = slice(0, 3 * T // 4)
+        copied = slice(3 * T // 4, T)
+        nc.sync.dma_start(m_new[2][:, loaded], m_planes[:, 2, loaded])
         nc.sync.dma_start(m_src[3][:], m_planes[:, 3, :])
-        nc.sync.dma_start(m_new[3][:, loaded], m_planes[:, 3, loaded])
+        nc.sync.dma_start(m_new[3][:], m_planes[:, 3, :])
 
         def scatter_on_scalar(window, values, part):
             nc.scalar.activation(listed(window, part), values, COPY)
@@ -177,29 +177,27 @@ def tile_attend_gsq_pl_nag_kernel(tc, xT, wT, y, wt, xm, mT, offs, out_0, out_1,
         gather(1)
         nc.vector.tensor_copy(m_new[1][:], m_src[1][:])
         nc.vector.tensor_tensor(sums[1], w_got[:, 1, :], steps[1], ADD)
-        momentum(m_val[:, 1, first], 1, first)
-        scatter_on_scalar(m_new[1], m_val[:, 1, first], first)
-        descend(sums[0][:, second], 1, first, sums[1][:, first])
-        scatter_on_scalar(w_new[1], sums[0][:, second], first)
-        momentum(m_val[:, 1, second], 1, second)
-        scatter_on_scalar(m_new[1], m_val[:, 1, second], second)
-        descend(w_got[:, 1, :], 2, whole[0], w_got[:, 2, :])
+        for part in halves:
+            momentum(m_val[:, 1, part], 1, part)
+            descend(w_got[:, 1, part], 1, part, sums[1][:, part])
+            scatter_on_scalar(m_new[1], m_val[:, 1, part], part)
+            scatter_on_scalar(w_new[1], w_got[:, 1, part], part)
+        descend(sums[1], 2, whole[0], w_got[:, 2, :])
         gather(2)
-        nc.vector.tensor_tensor(listed(w_new[2], whole[0]), w_got[:, 1, :], steps[2], ADD)
+        nc.vector.tensor_copy(m_new[2][:, copied], m_src[2][:, copied])
+        nc.vector.tensor_tensor(listed(w_new[2], whole[0]), sums[1], steps[2], ADD)
         momentum(m_val[:, 2, first], 2, first)
-        descend(w_got[:, 1, second], 1, second, sums[1][:, second])
-        scatter_on_scalar(w_new[1], w_got[:, 1, second], second)
         descend(sums[1], 3, whole[0], w_got[:, 3, :])
         scatter_on_scalar(m_new[2], m_val[:, 2, first], first)
         for part in halves:
             nc.vector.tensor_copy(steps[3][:, part], listed(m_src[3], part))
-        nc.scalar.activation(m_new[3][:, copied], m_src[3][:, copied], COPY)
         for part in halves:
             nc.vector.scalar_tensor_tensor(w_got[:, 3, part], steps[3][:, part], MOM_STEP, sums[1][:, part], MULT, ADD)
         momentum(sums[1][:, first], 2, second)
         nc.vector.tensor_copy(listed(w_new[3], whole[0]), w_got[:, 3, :])
         nc.vector.scalar_tensor_tensor(w_got[:, 3, :], steps[3], BETA, grad[3][:], MULT, ADD)
-        nc.scalar.activation(rounded[:, 3, T // 2 :], w_new[3][:, T // 2 :], COPY)
+        for part in (slice(T // 4, T // 2), slice(T // 2, T)):
+            nc.scalar.activation(rounded[:, 3, part], w_new[3][:, part], COPY)
         scatter_on_scalar(m_new[2], sums[1][:, first], second)
         for part in halves:
             scatter_on_scalar(m_new[3], w_got[:, 3, part], part)
@@ -209,7 +207,6 @@ def tile_attend_gsq_pl_nag_kernel(tc, xT, wT, y, wt, xm, mT, offs, out_0, out_1,
         for j, start, stop in ((0, 0, 1), (0, 1, 4), (0, 4, 8), (2, 0, 4), (2, 4, 8), (1, 0, 4), (1, 4, 8), (3, 0, 2)):
             part = slice(start * T // 8, stop * T // 8)
             nc.gpsimd.tensor_copy(rounded[:, j, part], w_new[j][:, part])
-        nc.vector.tensor_copy(rounded[:, 3, T // 4 : T // 2], w_new[3][:, T // 4 : T // 2])
         quarter = T // 4
         out_scales = keep.tile([P, quarter], U8, name="out_scales", align_bytes=64)
         out_codes = [keep.tile([P, width], U32, name=f"out_codes{k}", align_bytes=64) for k, width in enumerate((quarter,) * 4)]

@@ -37,7 +37,9 @@ def tile_attend_gsq_pl_nag_kernel(tc, xT, wT, y, wt, xm, mT, offs, out_0, out_1,
     words_out = out_2[0].rearrange("p t l -> p (t l)").bitcast(I32)
     scales_out = out_3[0].bitcast(I32)
     halves = [slice(0, N // 2), slice(N // 2, N)]
-    whole = [slice(0, N)]
+    first, second = halves
+    whole = slice(0, N)
+    quarter = T // 4
 
     with ExitStack() as ctx:
         keep = ctx.enter_context(tc.tile_pool(name="keep", bufs=1))
@@ -46,9 +48,9 @@ def tile_attend_gsq_pl_nag_kernel(tc, xT, wT, y, wt, xm, mT, offs, out_0, out_1,
         def listed(window, part):
             return window[:].indirect(offsets[:, part.start // 16 : part.stop // 16])
 
-        def quantise(name, grouped, fmt, widths, tag=None):
+        def quantise(name, grouped, fmt, widths):
             width = grouped.shape[1] // L
-            codes = keep.tile([P, width], U32, name=name + "_codes", tag=tag or name, align_bytes=64)
+            codes = keep.tile([P, width], U32, name=name + "_codes", align_bytes=64)
             scales = keep.tile([P, width], U8, name=name + "_scales", align_bytes=64)
             c = 0
             for step in widths:
@@ -61,14 +63,15 @@ def tile_attend_gsq_pl_nag_kernel(tc, xT, wT, y, wt, xm, mT, offs, out_0, out_1,
             out = dst[:].rearrange("p (j s t) -> p s t j", j=L, t=L)[:, :, :, tiles]
             copy(out, src)
 
-        def weave(dst, src):
-            nc.vector.tensor_copy(dst.rearrange("p (c i t) -> p c t i", i=4, t=L), src.rearrange("p t (c i) -> p c t i", i=4))
+        def weave(dst, src, copy):
+            copy(dst.rearrange("p (c i t) -> p c t i", i=4, t=L), src.rearrange("p t (c i) -> p c t i", i=4))
 
         offsets = keep.tile([P, N // 16], U16, name="offsets")
-        w_src = [keep.tile([P, T], F32, name=f"w_src{j}", tag=f"table{j}") for j in range(L)]
-        nc.sync.dma_start(w_src[0][:], w_planes[:, 0, :])
+        w_pair = keep.tile([P, 2 * T], F32, name="w_pair", tag="table0")
+        w_src = [w_pair[:, :T], w_pair[:, T:]] + [keep.tile([P, T], F32, name=f"w_src{j}", tag=f"table{j}") for j in (2, 3)]
+        nc.sync.dma_start(w_pair[:].rearrange("p (j t) -> p j t", j=2), w_planes[:, 0:2, :])
         nc.sync.dma_start(offsets[:], offs)
-        for j in range(1, L):
+        for j in (2, 3):
             nc.sync.dma_start(w_src[j][:], w_planes[:, j, :])
         x_raw = keep.tile([P, L, R], F32, name="x_raw")
         nc.sync.dma_start(x_raw[:], x_rows)
@@ -77,27 +80,30 @@ def tile_attend_gsq_pl_nag_kernel(tc, xT, wT, y, wt, xm, mT, offs, out_0, out_1,
         target_pairs = [keep.tile([P, 2, N], F32, name=f"target{u}", tag=f"y{u}") for u in range(2)]
         for u in range(2):
             nc.sync.dma_start(target_pairs[u][:], y_rows[:, 2 * u : 2 * u + 2, :])
-        scaled = keep.tile([P, 2, N], F32, name="scaled")
-        target = [scaled[:, 0, :], scaled[:, 1, :], target_pairs[1][:, 0, :], target_pairs[1][:, 1, :]]
         xm_raw = keep.tile([P, L, D], F32, name="xm_raw")
         nc.sync.dma_start(xm_raw[:], xm_rows)
-        m_src = [keep.tile([P, T], F32, name=f"m_src{j}") for j in range(L)]
+        m_src = [keep.tile([P, T], F32, name=f"m_src{j}", tag=f"mom{j}", align_bytes=64) for j in range(L)]
         w_new = [keep.tile([P, T], F32, name=f"w_new{j}") for j in range(L - 1)]
-        for j in range(L - 1):
+        for j in range(3):
             nc.sync.dma_start(m_src[j][:], m_planes[:, j, :])
 
         w_got = keep.tile([P, L, N], F32, name="w_got")
         w_bf = keep.tile([P, L * N], BF16, name="w_bf", align_bytes=64)
-        for j in range(L):
-            if j < L - 1:
-                nc.vector.tensor_copy(w_got[:, j, :], listed(w_src[j], whole[0]))
-                nc.scalar.activation(w_new[j][:], w_src[j][:], COPY)
-            else:
-                nc.vector.tensor_copy(w_got[:, j, halves[0]], listed(w_src[j], halves[0]))
-                nc.scalar.activation(w_got[:, j, halves[1]], listed(w_src[j], halves[1]), COPY)
-            if j % 2 == 1:
-                for part, copy in zip(halves, (nc.vector.tensor_copy, nc.scalar.copy)) if j == L - 1 else [(whole[0], nc.vector.tensor_copy)]:
-                    copy(w_bf[:].rearrange("p (n t) -> p n t", t=L)[:, part, j - 1 : j + 1], w_got[:, j - 1 : j + 1, part].rearrange("p t n -> p n t"))
+
+        def weave_pair(j, part, copy):
+            copy(w_bf[:].rearrange("p (n t) -> p n t", t=L)[:, part, j : j + 2], w_got[:, j : j + 2, part].rearrange("p t n -> p n t"))
+
+        nc.scalar.activation(w_new[0][:, : 3 * P], w_src[0][:, : 3 * P], COPY)
+        for j in range(L - 1):
+            nc.scalar.activation(w_got[:, j, :], listed(w_src[j], whole), COPY)
+            cols = slice(3 * P if j == 0 else 0, T)
+            nc.vector.tensor_copy(w_new[j][:, cols], w_src[j][:, cols])
+            if j == 1:
+                weave_pair(0, whole, nc.vector.tensor_copy)
+        nc.vector.tensor_copy(w_got[:, 3, first], listed(w_src[3], first))
+        nc.scalar.activation(w_got[:, 3, second], listed(w_src[3], second), COPY)
+        weave_pair(2, first, nc.vector.tensor_copy)
+        weave_pair(2, second, nc.scalar.copy)
         w_codes, w_scales = quantise("w", w_bf, E4M3, (256, 256))
         x_bf = keep.tile([P, L * R], BF16, name="x_bf", align_bytes=64)
         deal(x_bf, x_raw, slice(0, 2), nc.vector.tensor_copy)
@@ -105,48 +111,51 @@ def tile_attend_gsq_pl_nag_kernel(tc, xT, wT, y, wt, xm, mT, offs, out_0, out_1,
         x_codes, x_scales = quantise("x", x_bf, E4M3, (128, 128, 256))
 
         g_flat = keep.tile([P, L, N], BF16, name="g_flat")
+        target = []
         for j in range(L):
-            cols = slice(j * P, (j + 1) * P)
-            if j < 2:
-                nc.scalar.activation(target[j], target_pairs[0][:, j, :], COPY, scale=weight[:, j : j + 1])
+            raw = target_pairs[j // 2][:, j % 2, :]
+            if j >= 2:
+                nc.gpsimd.tensor_scalar(raw, raw, weight[:, j : j + 1], 0.0, MULT, ADD)
+                target.append(raw)
             else:
-                nc.gpsimd.tensor_scalar(target[j], target[j], weight[:, j : j + 1], 0.0, MULT, ADD)
-            for h, product in enumerate(halves if j == 0 else whole):
-                score = psum.tile([P, N], F32, name=f"score{j}_{h}", tag=f"score{j}" if h == 0 else "grad3")
-                nc.tensor.matmul_mx(out=score[:, product], lhsT=x_codes[:, cols].bitcast(E4M3), lhsT_scale=x_scales[:, cols], rhs=w_codes[:, product].bitcast(E4M3), rhs_scale=w_scales[:, product], start=True, stop=True)
-                for part in halves if j == L - 1 else [product]:
-                    nc.vector.scalar_tensor_tensor(g_flat[:, j, part], score[:, part], weight[:, j : j + 1], target[j][:, part], MULT, SUB)
+                target.append(keep.tile([P, N], F32, name=f"scaled{j}")[:])
+                nc.scalar.activation(target[j], raw, COPY, scale=weight[:, j : j + 1])
+        for j, part, tag in ((0, first, "score0"), (0, second, "grad3"), (1, whole, "score1"), (2, whole, "score2"), (3, whole, "score3")):
+            cols = slice(j * P, (j + 1) * P)
+            bank = psum.tile([P, N], F32, name=f"score{j}_{part.start}", tag=tag)
+            nc.tensor.matmul_mx(out=bank[:, part], lhsT=x_codes[:, cols].bitcast(E4M3), lhsT_scale=x_scales[:, cols], rhs=w_codes[:, part].bitcast(E4M3), rhs_scale=w_scales[:, part], start=True, stop=True)
+            for piece in halves if j == L - 1 else [part]:
+                nc.vector.scalar_tensor_tensor(g_flat[:, j, piece], bank[:, piece], weight[:, j : j + 1], target[j][:, piece], MULT, SUB)
         w_new.append(keep.tile([P, T], F32, name="w_new3", tag="y0"))
         nc.scalar.activation(w_new[L - 1][:], w_src[L - 1][:], COPY)
         g_bf = keep.tile([P, L * N], BF16, name="g_bf", align_bytes=64)
-        for part in halves:
-            weave(g_bf[:, L * part.start : L * part.stop], g_flat[:, :, part])
-        xm_bf = keep.tile([P, L * D], BF16, name="xm_bf", align_bytes=64)
-        deal(xm_bf, xm_raw, slice(0, 2), nc.scalar.copy)
+        for part, copy in zip(halves, (nc.vector.tensor_copy, nc.vector.tensor_copy)):
+            weave(g_bf[:, L * part.start : L * part.stop], g_flat[:, :, part], copy)
         g_codes, g_scales = quantise("g", g_bf, E5M2, (256, 256))
 
-        grad = []
-
-        def gradient_pair(u):
-            xm_codes, xm_scales = quantise(f"xm{u}", xm_bf[:, 2 * u * D : 2 * (u + 1) * D], E4M3, (256,), tag=None)
+        xm_bf = keep.tile([P, L * D], BF16, name="xm_bf", align_bytes=64)
+        grad = {}
+        for u in range(2):
+            deal(xm_bf, xm_raw, slice(2 * u, 2 * u + 2), nc.vector.tensor_copy if u else nc.scalar.copy)
+            xm_codes, xm_scales = quantise(f"xm{u}", xm_bf[:, 2 * u * D : 2 * (u + 1) * D], E4M3, (256,))
             for j in (2 * u, 2 * u + 1):
                 cols = slice((j % 2) * P, (j % 2 + 1) * P)
-                grad.append(psum.tile([P, N], F32, name=f"grad{j}", tag=f"grad{j}"))
-                nc.tensor.matmul_mx(out=grad[j][:], lhsT=xm_codes[:, cols].bitcast(E4M3), lhsT_scale=xm_scales[:, cols], rhs=g_codes[:].bitcast(E5M2), rhs_scale=g_scales[:], start=True, stop=True)
+                for h, part in enumerate([whole]):
+                    bank = psum.tile([P, N], F32, name=f"grad{j}_{h}", tag=f"grad{j}")
+                    nc.tensor.matmul_mx(out=bank[:, part], lhsT=xm_codes[:, cols].bitcast(E4M3), lhsT_scale=xm_scales[:, cols], rhs=g_codes[:, part].bitcast(E5M2), rhs_scale=g_scales[:, part], start=True, stop=True)
+                    grad[j, h] = bank
+        for j in range(L):
+            grad[j, 1] = grad[j, 0]
 
-        gradient_pair(0)
-        deal(xm_bf, xm_raw, slice(2, 4), nc.vector.tensor_copy)
-        gradient_pair(1)
-
-        first, second = halves
         flat = keep.tile([P, L * T], BF16, name="rounded")
         rounded = flat[:].rearrange("p (j t) -> p j t", j=L)
         m_val = keep.tile([P, L, N], F32, name="m_val")
-        steps = [flat[:, T + N : T + 3 * N].bitcast(F32) if j == 2 else keep.tile([P, N], F32, name=f"step{j}")[:] for j in range(L)]
-        sums = [keep.tile([P, N], F32, name=f"sum{j}")[:] for j in range(2)]
+        steps = [keep.tile([P, N], F32, name=f"step{j}")[:] for j in range(L)]
+        early = flat[:, : 2 * N].bitcast(F32)
+        late = flat[:, 2 * T - N : 2 * T + N].bitcast(F32)
         m_new = [keep.tile([P, T], F32, name=f"m_new{j}", tag=f"table{j}") for j in range(L)]
-        loaded = slice(0, 3 * T // 4)
-        copied = slice(3 * T // 4, T)
+        loaded = slice(0, 5 * T // 8)
+        copied = slice(5 * T // 8, T)
         nc.sync.dma_start(m_new[2][:, loaded], m_planes[:, 2, loaded])
         nc.sync.dma_start(m_src[3][:], m_planes[:, 3, :])
         nc.sync.dma_start(m_new[3][:], m_planes[:, 3, :])
@@ -155,65 +164,68 @@ def tile_attend_gsq_pl_nag_kernel(tc, xT, wT, y, wt, xm, mT, offs, out_0, out_1,
             nc.scalar.activation(listed(window, part), values, COPY)
 
         def gather(j):
-            nc.vector.tensor_scalar(steps[j], listed(m_src[j], whole[0]), MOM_STEP, 0.0, MULT, ADD)
+            nc.vector.tensor_scalar(steps[j], listed(m_src[j], whole), MOM_STEP, 0.0, MULT, ADD)
 
         def momentum(dst, j, part):
-            nc.vector.scalar_tensor_tensor(dst, steps[j][:, part], BETA / MOM_STEP, grad[j][:, part], MULT, ADD)
+            nc.vector.scalar_tensor_tensor(dst, steps[j][:, part], BETA / MOM_STEP, grad[j, part.start // (N // 2)][:, part], MULT, ADD)
 
         def descend(dst, j, part, src):
-            nc.vector.scalar_tensor_tensor(dst, grad[j][:, part], GRAD_STEP, src, MULT, ADD)
+            nc.vector.scalar_tensor_tensor(dst, grad[j, part.start // (N // 2)][:, part], GRAD_STEP, src, MULT, ADD)
 
-        nc.scalar.activation(steps[0], listed(m_src[0], whole[0]), COPY, scale=MOM_STEP)
+        nc.scalar.activation(steps[0], listed(m_src[0], whole), COPY, scale=MOM_STEP)
         nc.scalar.activation(m_new[0][:, : T // 2], m_src[0][:, : T // 2], COPY)
         nc.vector.tensor_copy(m_new[0][:, T // 2 :], m_src[0][:, T // 2 :])
-        nc.vector.tensor_tensor(sums[0], w_got[:, 0, :], steps[0], ADD)
-        momentum(m_val[:, 0, first], 0, first)
-        scatter_on_scalar(m_new[0], m_val[:, 0, first], first)
+        nc.vector.tensor_tensor(early, w_got[:, 0, :], steps[0], ADD)
         for part in halves:
-            descend(w_got[:, 0, part], 0, part, sums[0][:, part])
+            momentum(m_val[:, 0, part], 0, part)
+            descend(w_got[:, 0, part], 0, part, early[:, part])
+            scatter_on_scalar(m_new[0], m_val[:, 0, part], part)
             scatter_on_scalar(w_new[0], w_got[:, 0, part], part)
-        momentum(sums[0][:, first], 0, second)
-        scatter_on_scalar(m_new[0], sums[0][:, first], second)
+        descend(steps[0], 1, whole, w_got[:, 1, :])
+        descend(early, 2, whole, w_got[:, 2, :])
         gather(1)
         nc.vector.tensor_copy(m_new[1][:], m_src[1][:])
-        nc.vector.tensor_tensor(sums[1], w_got[:, 1, :], steps[1], ADD)
-        for part in halves:
-            momentum(m_val[:, 1, part], 1, part)
-            descend(w_got[:, 1, part], 1, part, sums[1][:, part])
-            scatter_on_scalar(m_new[1], m_val[:, 1, part], part)
-            scatter_on_scalar(w_new[1], w_got[:, 1, part], part)
-        descend(sums[1], 2, whole[0], w_got[:, 2, :])
+        new1 = keep.tile([P, N], F32, name="new1", tag="mom1", align_bytes=64)[:]
+        nc.gpsimd.tensor_tensor(new1, steps[0], steps[1], ADD)
+        momentum(m_val[:, 1, first], 1, first)
+        scatter_on_scalar(m_new[1], m_val[:, 1, first], first)
+        scatter_on_scalar(w_new[1], new1[:, first], first)
         gather(2)
         nc.vector.tensor_copy(m_new[2][:, copied], m_src[2][:, copied])
-        nc.vector.tensor_tensor(listed(w_new[2], whole[0]), sums[1], steps[2], ADD)
+        nc.vector.tensor_tensor(late, early, steps[2], ADD)
+        held = keep.tile([P, N // 2], F32, name="held", tag="mom2", align_bytes=64)[:]
+        momentum(held, 1, second)
+        scatter_on_scalar(w_new[1], new1[:, second], second)
+        scatter_on_scalar(m_new[1], held, second)
+        nc.vector.tensor_copy(listed(w_new[2], whole), late)
         momentum(m_val[:, 2, first], 2, first)
-        descend(sums[1], 3, whole[0], w_got[:, 3, :])
+        descend(late, 3, whole, w_got[:, 3, :])
         scatter_on_scalar(m_new[2], m_val[:, 2, first], first)
         for part in halves:
             nc.vector.tensor_copy(steps[3][:, part], listed(m_src[3], part))
         for part in halves:
-            nc.vector.scalar_tensor_tensor(w_got[:, 3, part], steps[3][:, part], MOM_STEP, sums[1][:, part], MULT, ADD)
-        momentum(sums[1][:, first], 2, second)
-        nc.vector.tensor_copy(listed(w_new[3], whole[0]), w_got[:, 3, :])
-        nc.vector.scalar_tensor_tensor(w_got[:, 3, :], steps[3], BETA, grad[3][:], MULT, ADD)
+            nc.vector.scalar_tensor_tensor(w_got[:, 3, part], steps[3][:, part], MOM_STEP, late[:, part], MULT, ADD)
+        kept = keep.tile([P, N // 2], F32, name="kept", tag="mom3", align_bytes=64)[:]
+        momentum(kept, 2, second)
+        nc.vector.tensor_copy(listed(w_new[3], whole), w_got[:, 3, :])
+        nc.vector.scalar_tensor_tensor(w_got[:, 3, :], steps[3], BETA, grad[3, 0][:], MULT, ADD)
         for part in (slice(T // 4, T // 2), slice(T // 2, T)):
             nc.scalar.activation(rounded[:, 3, part], w_new[3][:, part], COPY)
-        scatter_on_scalar(m_new[2], sums[1][:, first], second)
+        scatter_on_scalar(m_new[2], kept, second)
         for part in halves:
             scatter_on_scalar(m_new[3], w_got[:, 3, part], part)
-        for planes, tables, j in ((o1_planes, m_new, 0), (o0_planes, w_new, 0), (o0_planes, w_new, 2), (o1_planes, m_new, 1), (o0_planes, w_new, 1), (o0_planes, w_new, 3), (o1_planes, m_new, 2)):
+        for planes, tables, j in ((o1_planes, m_new, 0), (o0_planes, w_new, 0), (o0_planes, w_new, 2), (o0_planes, w_new, 1), (o1_planes, m_new, 1), (o0_planes, w_new, 3), (o1_planes, m_new, 2)):
             nc.sync.dma_start(planes[:, j, :], tables[j][:])
 
-        for j, start, stop in ((0, 0, 1), (0, 1, 4), (0, 4, 8), (2, 0, 4), (2, 4, 8), (1, 0, 4), (1, 4, 8), (3, 0, 2)):
+        for j, start, stop in ((0, 0, 8), (2, 2, 8), (2, 0, 2), (1, 0, 8), (3, 0, 2)):
             part = slice(start * T // 8, stop * T // 8)
             nc.gpsimd.tensor_copy(rounded[:, j, part], w_new[j][:, part])
-        quarter = T // 4
         out_scales = keep.tile([P, quarter], U8, name="out_scales", align_bytes=64)
         out_codes = [keep.tile([P, width], U32, name=f"out_codes{k}", align_bytes=64) for k, width in enumerate((quarter,) * 4)]
         for q in range(4):
             cols = slice(q * quarter, (q + 1) * quarter)
             out_bf = keep.tile([P, L * quarter], BF16, name=f"out_bf{q}", align_bytes=64)
-            weave(out_bf[:], rounded[:, :, cols])
+            weave(out_bf[:], rounded[:, :, cols], nc.vector.tensor_copy)
             nc.vector.quantize_mx(out=out_codes[q][:].bitcast(E4M3), scales=out_scales[4 * q :, :], in_=out_bf[:])
             nc.sync.dma_start(words_out[:, cols], out_codes[q][:].bitcast(I32))
             if q == 1:

@@ -43,14 +43,16 @@ def tile_attend_gsq_pl_nag_kernel(tc, xT, wT, y, wt, xm, mT, offs, out_0, out_1,
 
     with ExitStack() as ctx:
         keep = ctx.enter_context(tc.tile_pool(name="keep", bufs=1))
+        shared = ctx.enter_context(tc.tile_pool(name="shared", bufs=1))
         psum = ctx.enter_context(tc.psum_pool(name="psum", bufs=1))
 
         def listed(window, part):
             return window[:].indirect(offsets[:, part.start // 16 : part.stop // 16])
 
-        def quantise(name, grouped, fmt, widths):
+        def quantise(name, grouped, fmt, widths, codes=None):
             width = grouped.shape[1] // L
-            codes = keep.tile([P, width], U32, name=name + "_codes", align_bytes=64)
+            if codes is None:
+                codes = keep.tile([P, width], U32, name=name + "_codes", align_bytes=64)
             scales = keep.tile([P, width], U8, name=name + "_scales", align_bytes=64)
             c = 0
             for step in widths:
@@ -82,7 +84,7 @@ def tile_attend_gsq_pl_nag_kernel(tc, xT, wT, y, wt, xm, mT, offs, out_0, out_1,
             nc.sync.dma_start(target_pairs[u][:], y_rows[:, 2 * u : 2 * u + 2, :])
         xm_raw = keep.tile([P, L, D], F32, name="xm_raw")
         nc.sync.dma_start(xm_raw[:], xm_rows)
-        m_src = [keep.tile([P, T], F32, name=f"m_src{j}", tag=f"mom{j}", align_bytes=64) for j in range(L)]
+        m_src = [shared.tile([P, T], F32, name="m_src0", offset=15 * 1024, align_bytes=64)] + [keep.tile([P, T], F32, name=f"m_src{j}", tag=f"mom{j}", align_bytes=64) for j in range(1, L)]
         w_new = [keep.tile([P, T], F32, name=f"w_new{j}") for j in range(L - 1)]
         for j in range(3):
             nc.sync.dma_start(m_src[j][:], m_planes[:, j, :])
@@ -136,23 +138,22 @@ def tile_attend_gsq_pl_nag_kernel(tc, xT, wT, y, wt, xm, mT, offs, out_0, out_1,
         xm_bf = keep.tile([P, L * D], BF16, name="xm_bf", align_bytes=64)
         grad = {}
         for u in range(2):
-            deal(xm_bf, xm_raw, slice(2 * u, 2 * u + 2), nc.vector.tensor_copy if u else nc.scalar.copy)
-            xm_codes, xm_scales = quantise(f"xm{u}", xm_bf[:, 2 * u * D : 2 * (u + 1) * D], E4M3, (256,))
+            deal(xm_bf, xm_raw, slice(2 * u, 2 * u + 2), nc.scalar.copy)
+
+        def gradient_pair(u, codes):
+            xm_codes, xm_scales = quantise(f"xm{u}", xm_bf[:, 2 * u * D : 2 * (u + 1) * D], E4M3, (256,), codes)
             for j in (2 * u, 2 * u + 1):
                 cols = slice((j % 2) * P, (j % 2 + 1) * P)
-                for h, part in enumerate([whole]):
-                    bank = psum.tile([P, N], F32, name=f"grad{j}_{h}", tag=f"grad{j}")
+                for h, part in enumerate(halves if j == 0 else [whole]):
+                    bank = psum.tile([P, N], F32, name=f"grad{j}_{h}", tag="score0" if j + h == 0 else f"grad{j}")
                     nc.tensor.matmul_mx(out=bank[:, part], lhsT=xm_codes[:, cols].bitcast(E4M3), lhsT_scale=xm_scales[:, cols], rhs=g_codes[:, part].bitcast(E5M2), rhs_scale=g_scales[:, part], start=True, stop=True)
                     grad[j, h] = bank
-        for j in range(L):
-            grad[j, 1] = grad[j, 0]
+                grad[j, 1] = bank
 
-        flat = keep.tile([P, L * T], BF16, name="rounded")
-        rounded = flat[:].rearrange("p (j t) -> p j t", j=L)
+        gradient_pair(0, None)
+
         m_val = keep.tile([P, L, N], F32, name="m_val")
         steps = [keep.tile([P, N], F32, name=f"step{j}")[:] for j in range(L)]
-        early = flat[:, : 2 * N].bitcast(F32)
-        late = flat[:, 2 * T - N : 2 * T + N].bitcast(F32)
         m_new = [keep.tile([P, T], F32, name=f"m_new{j}", tag=f"table{j}") for j in range(L)]
         loaded = slice(0, 5 * T // 8)
         copied = slice(5 * T // 8, T)
@@ -172,21 +173,31 @@ def tile_attend_gsq_pl_nag_kernel(tc, xT, wT, y, wt, xm, mT, offs, out_0, out_1,
         def descend(dst, j, part, src):
             nc.vector.scalar_tensor_tensor(dst, grad[j, part.start // (N // 2)][:, part], GRAD_STEP, src, MULT, ADD)
 
-        nc.scalar.activation(steps[0], listed(m_src[0], whole), COPY, scale=MOM_STEP)
-        nc.scalar.activation(m_new[0][:, : T // 2], m_src[0][:, : T // 2], COPY)
-        nc.vector.tensor_copy(m_new[0][:, T // 2 :], m_src[0][:, T // 2 :])
-        nc.vector.tensor_tensor(early, w_got[:, 0, :], steps[0], ADD)
         for part in halves:
-            momentum(m_val[:, 0, part], 0, part)
-            descend(w_got[:, 0, part], 0, part, early[:, part])
-            scatter_on_scalar(m_new[0], m_val[:, 0, part], part)
-            scatter_on_scalar(w_new[0], w_got[:, 0, part], part)
-        descend(steps[0], 1, whole, w_got[:, 1, :])
+            nc.scalar.activation(steps[0][:, part], listed(m_src[0], part), COPY, scale=MOM_STEP)
+        nc.vector.tensor_copy(m_new[0][:], m_src[0][:])
+        flat = shared.tile([P, L * T], BF16, name="rounded", offset=0, align_bytes=64)
+        rounded = flat[:].rearrange("p (j t) -> p j t", j=L)
+        early = flat[:, : 2 * N].bitcast(F32)
+        spare = flat[:, 3 * T : 3 * T + 2 * N].bitcast(F32)
+        late = flat[:, 2 * T - N : 2 * T + N].bitcast(F32)
+        momentum(m_val[:, 0, first], 0, first)
+        for part, term in zip(halves, (early, late)):
+            descend(term[:, part], 0, part, w_got[:, 0, part])
+        nc.gpsimd.tensor_tensor(w_got[:, 0, first], early[:, first], steps[0][:, first], ADD)
+        gradient_pair(1, shared.tile([P, 2 * P], U32, name="xm1_codes", offset=20 * 1024, align_bytes=64))
+        momentum(m_val[:, 0, second], 0, second)
+        nc.gpsimd.tensor_tensor(steps[0][:, second], late[:, second], steps[0][:, second], ADD)
+        descend(spare, 1, whole, w_got[:, 1, :])
+        scatter_on_scalar(m_new[0], m_val[:, 0, first], first)
+        scatter_on_scalar(w_new[0], w_got[:, 0, first], first)
+        scatter_on_scalar(m_new[0], m_val[:, 0, second], second)
+        scatter_on_scalar(w_new[0], steps[0][:, second], second)
         descend(early, 2, whole, w_got[:, 2, :])
         gather(1)
         nc.vector.tensor_copy(m_new[1][:], m_src[1][:])
         new1 = keep.tile([P, N], F32, name="new1", tag="mom1", align_bytes=64)[:]
-        nc.gpsimd.tensor_tensor(new1, steps[0], steps[1], ADD)
+        nc.gpsimd.tensor_tensor(new1, spare, steps[1], ADD)
         momentum(m_val[:, 1, first], 1, first)
         scatter_on_scalar(m_new[1], m_val[:, 1, first], first)
         scatter_on_scalar(w_new[1], new1[:, first], first)
@@ -225,7 +236,12 @@ def tile_attend_gsq_pl_nag_kernel(tc, xT, wT, y, wt, xm, mT, offs, out_0, out_1,
         for q in range(4):
             cols = slice(q * quarter, (q + 1) * quarter)
             out_bf = keep.tile([P, L * quarter], BF16, name=f"out_bf{q}", align_bytes=64)
-            weave(out_bf[:], rounded[:, :, cols], nc.vector.tensor_copy)
+            if q < 3:
+                weave(out_bf[:], rounded[:, :, cols], nc.vector.tensor_copy)
+            else:
+                middle = cols.start + quarter // 2
+                weave(out_bf[:, : 2 * quarter], rounded[:, :, cols.start : middle], nc.vector.tensor_copy)
+                weave(out_bf[:, 2 * quarter :], rounded[:, :, middle : cols.stop], nc.scalar.copy)
             nc.vector.quantize_mx(out=out_codes[q][:].bitcast(E4M3), scales=out_scales[4 * q :, :], in_=out_bf[:])
             nc.sync.dma_start(words_out[:, cols], out_codes[q][:].bitcast(I32))
             if q == 1:

@@ -86,7 +86,9 @@ def tile_attend_gsq_pl_nag_kernel(tc, xT, wT, y, wt, xm, mT, offs, out_0, out_1,
         nc.sync.dma_start(xm_raw[:], xm_rows)
         m_src = [shared.tile([P, T], F32, name="m_src0", offset=15 * 1024, align_bytes=64)] + [keep.tile([P, T], F32, name=f"m_src{j}", tag=f"mom{j}", align_bytes=64) for j in range(1, L)]
         w_new = [keep.tile([P, T], F32, name=f"w_new{j}") for j in range(L - 1)]
-        for j in range(3):
+        for cols in (slice(0, T // 2), slice(T // 2, T)):
+            nc.sync.dma_start(m_src[0][:, cols], m_planes[:, 0, cols])
+        for j in (1, 2):
             nc.sync.dma_start(m_src[j][:], m_planes[:, j, :])
 
         w_got = keep.tile([P, L, N], F32, name="w_got")
@@ -137,8 +139,7 @@ def tile_attend_gsq_pl_nag_kernel(tc, xT, wT, y, wt, xm, mT, offs, out_0, out_1,
 
         xm_bf = keep.tile([P, L * D], BF16, name="xm_bf", align_bytes=64)
         grad = {}
-        for u in range(2):
-            deal(xm_bf, xm_raw, slice(2 * u, 2 * u + 2), nc.scalar.copy)
+        deal(xm_bf, xm_raw, slice(0, 2), nc.scalar.copy)
 
         def gradient_pair(u, codes):
             xm_codes, xm_scales = quantise(f"xm{u}", xm_bf[:, 2 * u * D : 2 * (u + 1) * D], E4M3, (256,), codes)
@@ -151,6 +152,8 @@ def tile_attend_gsq_pl_nag_kernel(tc, xT, wT, y, wt, xm, mT, offs, out_0, out_1,
                 grad[j, 1] = bank
 
         gradient_pair(0, None)
+        deal(xm_bf, xm_raw, slice(2, 4), nc.vector.tensor_copy)
+        gradient_pair(1, None)
 
         m_val = keep.tile([P, L, N], F32, name="m_val")
         steps = [keep.tile([P, N], F32, name=f"step{j}")[:] for j in range(L)]
@@ -173,9 +176,10 @@ def tile_attend_gsq_pl_nag_kernel(tc, xT, wT, y, wt, xm, mT, offs, out_0, out_1,
         def descend(dst, j, part, src):
             nc.vector.scalar_tensor_tensor(dst, grad[j, part.start // (N // 2)][:, part], GRAD_STEP, src, MULT, ADD)
 
+        nc.scalar.activation(m_new[0][:, : T // 2], m_src[0][:, : T // 2], COPY)
         for part in halves:
             nc.scalar.activation(steps[0][:, part], listed(m_src[0], part), COPY, scale=MOM_STEP)
-        nc.vector.tensor_copy(m_new[0][:], m_src[0][:])
+        nc.vector.tensor_copy(m_new[0][:, T // 2 :], m_src[0][:, T // 2 :])
         flat = shared.tile([P, L * T], BF16, name="rounded", offset=0, align_bytes=64)
         rounded = flat[:].rearrange("p (j t) -> p j t", j=L)
         early = flat[:, : 2 * N].bitcast(F32)
@@ -185,7 +189,6 @@ def tile_attend_gsq_pl_nag_kernel(tc, xT, wT, y, wt, xm, mT, offs, out_0, out_1,
         for part, term in zip(halves, (early, late)):
             descend(term[:, part], 0, part, w_got[:, 0, part])
         nc.gpsimd.tensor_tensor(w_got[:, 0, first], early[:, first], steps[0][:, first], ADD)
-        gradient_pair(1, shared.tile([P, 2 * P], U32, name="xm1_codes", offset=20 * 1024, align_bytes=64))
         momentum(m_val[:, 0, second], 0, second)
         nc.gpsimd.tensor_tensor(steps[0][:, second], late[:, second], steps[0][:, second], ADD)
         descend(spare, 1, whole, w_got[:, 1, :])
@@ -236,12 +239,7 @@ def tile_attend_gsq_pl_nag_kernel(tc, xT, wT, y, wt, xm, mT, offs, out_0, out_1,
         for q in range(4):
             cols = slice(q * quarter, (q + 1) * quarter)
             out_bf = keep.tile([P, L * quarter], BF16, name=f"out_bf{q}", align_bytes=64)
-            if q < 3:
-                weave(out_bf[:], rounded[:, :, cols], nc.vector.tensor_copy)
-            else:
-                middle = cols.start + quarter // 2
-                weave(out_bf[:, : 2 * quarter], rounded[:, :, cols.start : middle], nc.vector.tensor_copy)
-                weave(out_bf[:, 2 * quarter :], rounded[:, :, middle : cols.stop], nc.scalar.copy)
+            weave(out_bf[:], rounded[:, :, cols], nc.vector.tensor_copy)
             nc.vector.quantize_mx(out=out_codes[q][:].bitcast(E4M3), scales=out_scales[4 * q :, :], in_=out_bf[:])
             nc.sync.dma_start(words_out[:, cols], out_codes[q][:].bitcast(I32))
             if q == 1:

@@ -158,8 +158,8 @@ def tile_attend_gsq_pl_nag_kernel(tc, xT, wT, y, wt, xm, mT, offs, out_0, out_1,
         m_val = keep.tile([P, L, N], F32, name="m_val")
         steps = [keep.tile([P, N], F32, name=f"step{j}")[:] for j in range(L)]
         m_new = [keep.tile([P, T], F32, name=f"m_new{j}", tag=f"table{j}") for j in range(L)]
-        loaded = slice(0, 5 * T // 8)
-        copied = slice(5 * T // 8, T)
+        loaded = slice(0, T // 2)
+        copied = slice(T // 2, T)
         nc.sync.dma_start(m_new[2][:, loaded], m_planes[:, 2, loaded])
         nc.sync.dma_start(m_src[3][:], m_planes[:, 3, :])
         nc.sync.dma_start(m_new[3][:], m_planes[:, 3, :])
@@ -177,23 +177,25 @@ def tile_attend_gsq_pl_nag_kernel(tc, xT, wT, y, wt, xm, mT, offs, out_0, out_1,
             nc.vector.scalar_tensor_tensor(dst, grad[j, part.start // (N // 2)][:, part], GRAD_STEP, src, MULT, ADD)
 
         nc.scalar.activation(m_new[0][:, : T // 2], m_src[0][:, : T // 2], COPY)
-        for part in halves:
-            nc.scalar.activation(steps[0][:, part], listed(m_src[0], part), COPY, scale=MOM_STEP)
+        for part, scale in zip(halves, (LR * BETA / GRAD_STEP, MOM_STEP)):
+            nc.scalar.activation(steps[0][:, part], listed(m_src[0], part), COPY, scale=scale)
+        over_step = target[2][:, first]
+        nc.gpsimd.tensor_scalar(over_step, w_got[:, 0, first], 1.0 / GRAD_STEP, 0.0, MULT, ADD)
         nc.vector.tensor_copy(m_new[0][:, T // 2 :], m_src[0][:, T // 2 :])
         flat = shared.tile([P, L * T], BF16, name="rounded", offset=0, align_bytes=64)
         rounded = flat[:].rearrange("p (j t) -> p j t", j=L)
         early = flat[:, : 2 * N].bitcast(F32)
         spare = flat[:, 3 * T : 3 * T + 2 * N].bitcast(F32)
         late = flat[:, 2 * T - N : 2 * T + N].bitcast(F32)
-        momentum(m_val[:, 0, first], 0, first)
-        for part, term in zip(halves, (early, late)):
-            descend(term[:, part], 0, part, w_got[:, 0, part])
-        nc.gpsimd.tensor_tensor(w_got[:, 0, first], early[:, first], steps[0][:, first], ADD)
+        nc.vector.scalar_tensor_tensor(m_val[:, 0, first], steps[0][:, first], GRAD_STEP / LR, grad[0, 0][:, first], MULT, ADD)
+        descend(late[:, second], 0, second, w_got[:, 0, second])
+        nc.gpsimd.tensor_tensor(late[:, first], over_step, steps[0][:, first], ADD)
+        nc.gpsimd.tensor_tensor(w_got[:, 0, first], late[:, first], m_val[:, 0, first], ADD)
         momentum(m_val[:, 0, second], 0, second)
         nc.gpsimd.tensor_tensor(steps[0][:, second], late[:, second], steps[0][:, second], ADD)
         descend(spare, 1, whole, w_got[:, 1, :])
         scatter_on_scalar(m_new[0], m_val[:, 0, first], first)
-        scatter_on_scalar(w_new[0], w_got[:, 0, first], first)
+        nc.scalar.activation(listed(w_new[0], first), w_got[:, 0, first], COPY, scale=GRAD_STEP)
         scatter_on_scalar(m_new[0], m_val[:, 0, second], second)
         scatter_on_scalar(w_new[0], steps[0][:, second], second)
         descend(early, 2, whole, w_got[:, 2, :])
@@ -223,8 +225,8 @@ def tile_attend_gsq_pl_nag_kernel(tc, xT, wT, y, wt, xm, mT, offs, out_0, out_1,
         momentum(kept, 2, second)
         nc.vector.tensor_copy(listed(w_new[3], whole), w_got[:, 3, :])
         nc.vector.scalar_tensor_tensor(w_got[:, 3, :], steps[3], BETA, grad[3, 0][:], MULT, ADD)
-        for part in (slice(T // 4, T // 2), slice(T // 2, T)):
-            nc.scalar.activation(rounded[:, 3, part], w_new[3][:, part], COPY)
+        nc.vector.tensor_copy(rounded[:, 3, quarter : 2 * quarter], w_new[3][:, quarter : 2 * quarter])
+        nc.scalar.activation(rounded[:, 3, 2 * quarter :], w_new[3][:, 2 * quarter :], COPY)
         scatter_on_scalar(m_new[2], kept, second)
         for part in halves:
             scatter_on_scalar(m_new[3], w_got[:, 3, part], part)

@@ -97,10 +97,10 @@ def tile_attend_gsq_pl_nag_kernel(tc, xT, wT, y, wt, xm, mT, offs, out_0, out_1,
         def weave_pair(j, part, copy):
             copy(w_bf[:].rearrange("p (n t) -> p n t", t=L)[:, part, j : j + 2], w_got[:, j : j + 2, part].rearrange("p t n -> p n t"))
 
-        nc.scalar.activation(w_new[0][:, : 3 * P], w_src[0][:, : 3 * P], COPY)
+        nc.scalar.activation(w_new[0][:, : 2 * P], w_src[0][:, : 2 * P], COPY)
         for j in range(L - 1):
             nc.scalar.activation(w_got[:, j, :], listed(w_src[j], whole), COPY)
-            cols = slice(3 * P if j == 0 else 0, T)
+            cols = slice(2 * P if j == 0 else 0, T)
             nc.vector.tensor_copy(w_new[j][:, cols], w_src[j][:, cols])
             if j == 1:
                 weave_pair(0, whole, nc.vector.tensor_copy)
@@ -179,8 +179,8 @@ def tile_attend_gsq_pl_nag_kernel(tc, xT, wT, y, wt, xm, mT, offs, out_0, out_1,
         nc.scalar.activation(m_new[0][:, : T // 2], m_src[0][:, : T // 2], COPY)
         for part, scale in zip(halves, (LR * BETA / GRAD_STEP, MOM_STEP)):
             nc.scalar.activation(steps[0][:, part], listed(m_src[0], part), COPY, scale=scale)
-        over_step = target[2][:, first]
-        nc.gpsimd.tensor_scalar(over_step, w_got[:, 0, first], 1.0 / GRAD_STEP, 0.0, MULT, ADD)
+        over_step = keep.tile([P, N // 2], F32, name="over_step")[:]
+        nc.scalar.activation(over_step, w_got[:, 0, first], COPY, scale=1.0 / GRAD_STEP)
         nc.vector.tensor_copy(m_new[0][:, T // 2 :], m_src[0][:, T // 2 :])
         flat = shared.tile([P, L * T], BF16, name="rounded", offset=0, align_bytes=64)
         rounded = flat[:].rearrange("p (j t) -> p j t", j=L)
@@ -233,7 +233,7 @@ def tile_attend_gsq_pl_nag_kernel(tc, xT, wT, y, wt, xm, mT, offs, out_0, out_1,
         for planes, tables, j in ((o1_planes, m_new, 0), (o0_planes, w_new, 0), (o0_planes, w_new, 2), (o0_planes, w_new, 1), (o1_planes, m_new, 1), (o0_planes, w_new, 3), (o1_planes, m_new, 2)):
             nc.sync.dma_start(planes[:, j, :], tables[j][:])
 
-        for j, start, stop in ((0, 0, 8), (2, 2, 8), (2, 0, 2), (1, 0, 8), (3, 0, 2)):
+        for j, start, stop in ((0, 0, 8), (2, 3, 8), (2, 0, 3), (1, 0, 8), (3, 0, 2)):
             part = slice(start * T // 8, stop * T // 8)
             nc.gpsimd.tensor_copy(rounded[:, j, part], w_new[j][:, part])
         out_scales = keep.tile([P, quarter], U8, name="out_scales", align_bytes=64)

from contextlib import ExitStack

import concourse.mybir as mybir

N, T, D, R = 512, 2048, 512, 512
LR, BETA = 0.1, 0.9
FLOPS = 4 * R * D * N

F32 = mybir.dt.float32
BF16 = mybir.dt.bfloat16
I32 = mybir.dt.int32
U32 = mybir.dt.uint32
U16 = mybir.dt.uint16
U8 = mybir.dt.uint8
E4M3 = mybir.dt.float8_e4m3fn_x4
E5M2 = mybir.dt.float8_e5m2_x4
MULT = mybir.AluOpType.mult
ADD = mybir.AluOpType.add
SUB = mybir.AluOpType.subtract
COPY = mybir.ActivationFunctionType.Copy

P = 128
L = 4
GRAD_STEP = -LR * (1.0 + BETA)
MOM_STEP = -LR * BETA * BETA


def tile_attend_gsq_pl_nag_kernel(tc, xT, wT, y, wt, xm, mT, offs, out_0, out_1, out_2, out_3):
    nc = tc.nc
    w_planes = wT.rearrange("(p j) t -> p j t", j=L)
    m_planes = mT.rearrange("(p j) t -> p j t", j=L)
    o0_planes = out_0.rearrange("(p j) t -> p j t", j=L)
    o1_planes = out_1.rearrange("(p j) t -> p j t", j=L)
    x_rows = xT[0].rearrange("(p j) r -> p j r", j=L)
    xm_rows = xm[0].rearrange("(p j) d -> p j d", j=L)
    y_rows = y[0].rearrange("(p j) n -> p j n", j=L)
    words_out = out_2[0].rearrange("p t l -> p (t l)").bitcast(I32)
    scales_out = out_3[0].bitcast(I32)
    halves = [slice(0, N // 2), slice(N // 2, N)]
    first, second = halves
    whole = slice(0, N)
    quarter = T // 4

    with ExitStack() as ctx:
        keep = ctx.enter_context(tc.tile_pool(name="keep", bufs=1))
        shared = ctx.enter_context(tc.tile_pool(name="shared", bufs=1))
        psum = ctx.enter_context(tc.psum_pool(name="psum", bufs=1))

        def listed(window, part):
            return window[:].indirect(offsets[:, part.start // 16 : part.stop // 16])

        def quantise(name, grouped, fmt, widths, codes=None):
            width = grouped.shape[1] // L
            if codes is None:
                codes = keep.tile([P, width], U32, name=name + "_codes", align_bytes=64)
            scales = keep.tile([P, width], U8, name=name + "_scales", align_bytes=64)
            c = 0
            for step in widths:
                nc.vector.quantize_mx(out=codes[:, c : c + step].bitcast(fmt), scales=scales[:, c : c + step], in_=grouped[:, L * c : L * (c + step)])
                c = c + step
            return codes, scales

        def deal(dst, raw, tiles, copy):
            src = raw[:].rearrange("p t (s j) -> p s t j", j=L)[:, :, :, tiles]
            out = dst[:].rearrange("p (j s t) -> p s t j", j=L, t=L)[:, :, :, tiles]
            copy(out, src)

        def weave(dst, src, copy):
            copy(dst.rearrange("p (c i t) -> p c t i", i=4, t=L), src.rearrange("p t (c i) -> p c t i", i=4))

        offsets = keep.tile([P, N // 16], U16, name="offsets")
        w_pair = keep.tile([P, 2 * T], F32, name="w_pair", tag="table0")
        w_src = [w_pair[:, :T], w_pair[:, T:]] + [keep.tile([P, T], F32, name=f"w_src{j}", tag=f"table{j}") for j in (2, 3)]
        nc.sync.dma_start(w_pair[:].rearrange("p (j t) -> p j t", j=2), w_planes[:, 0:2, :])
        nc.sync.dma_start(offsets[:], offs)
        for j in (2, 3):
            nc.sync.dma_start(w_src[j][:], w_planes[:, j, :])
        x_raw = keep.tile([P, L, R], F32, name="x_raw")
        nc.sync.dma_start(x_raw[:], x_rows)
        weight = keep.tile([P, L], F32, name="weight")
        nc.sync.dma_start(weight[:], wt[0].rearrange("(p j) o -> p (j o)", j=L))
        target_pairs = [keep.tile([P, 2, N], F32, name=f"target{u}", tag=f"y{u}") for u in range(2)]
        for u in range(2):
            nc.sync.dma_start(target_pairs[u][:], y_rows[:, 2 * u : 2 * u + 2, :])
        xm_raw = keep.tile([P, L, D], F32, name="xm_raw")
        nc.sync.dma_start(xm_raw[:], xm_rows)
        m_src = [shared.tile([P, T], F32, name="m_src0", offset=15 * 1024, align_bytes=64)] + [keep.tile([P, T], F32, name=f"m_src{j}", tag=f"mom{j}", align_bytes=64) for j in range(1, L)]
        w_new = [keep.tile([P, T], F32, name=f"w_new{j}") for j in range(L - 1)]
        for cols in (slice(0, T // 2), slice(T // 2, T)):
            nc.sync.dma_start(m_src[0][:, cols], m_planes[:, 0, cols])
        for j in (1, 2):
            nc.sync.dma_start(m_src[j][:], m_planes[:, j, :])

        w_got = keep.tile([P, L, N], F32, name="w_got")
        w_bf = keep.tile([P, L * N], BF16, name="w_bf", align_bytes=64)

        def weave_pair(j, part, copy):
            copy(w_bf[:].rearrange("p (n t) -> p n t", t=L)[:, part, j : j + 2], w_got[:, j : j + 2, part].rearrange("p t n -> p n t"))

        nc.scalar.activation(w_new[0][:, : 2 * P], w_src[0][:, : 2 * P], COPY)
        for j in range(L - 1):
            nc.scalar.activation(w_got[:, j, :], listed(w_src[j], whole), COPY)
            cols = slice(2 * P if j == 0 else 0, T)
            nc.vector.tensor_copy(w_new[j][:, cols], w_src[j][:, cols])
            if j == 1:
                weave_pair(0, whole, nc.vector.tensor_copy)
        nc.vector.tensor_copy(w_got[:, 3, first], listed(w_src[3], first))
        nc.scalar.activation(w_got[:, 3, second], listed(w_src[3], second), COPY)
        weave_pair(2, first, nc.vector.tensor_copy)
        weave_pair(2, second, nc.scalar.copy)
        w_codes, w_scales = quantise("w", w_bf, E4M3, (256, 256))
        x_bf = keep.tile([P, L * R], BF16, name="x_bf", align_bytes=64)
        deal(x_bf, x_raw, slice(0, 2), nc.vector.tensor_copy)
        deal(x_bf, x_raw, slice(2, 4), nc.scalar.copy)
        x_codes, x_scales = quantise("x", x_bf, E4M3, (128, 128, 256))

        g_flat = keep.tile([P, L, N], BF16, name="g_flat")
        target = []
        for j in range(L):
            raw = target_pairs[j // 2][:, j % 2, :]
            if j >= 2:
                nc.gpsimd.tensor_scalar(raw, raw, weight[:, j : j + 1], 0.0, MULT, ADD)
                target.append(raw)
            else:
                target.append(keep.tile([P, N], F32, name=f"scaled{j}")[:])
                nc.scalar.activation(target[j], raw, COPY, scale=weight[:, j : j + 1])
        for j, part, tag in ((0, first, "score0"), (0, second, "grad3"), (1, whole, "score1"), (2, whole, "score2"), (3, whole, "score3")):
            cols = slice(j * P, (j + 1) * P)
            bank = psum.tile([P, N], F32, name=f"score{j}_{part.start}", tag=tag)
            nc.tensor.matmul_mx(out=bank[:, part], lhsT=x_codes[:, cols].bitcast(E4M3), lhsT_scale=x_scales[:, cols], rhs=w_codes[:, part].bitcast(E4M3), rhs_scale=w_scales[:, part], start=True, stop=True)
            for piece in halves if j == L - 1 else [part]:
                nc.vector.scalar_tensor_tensor(g_flat[:, j, piece], bank[:, piece], weight[:, j : j + 1], target[j][:, piece], MULT, SUB)
        w_new.append(keep.tile([P, T], F32, name="w_new3", tag="y0"))
        nc.scalar.activation(w_new[L - 1][:], w_src[L - 1][:], COPY)
        g_bf = keep.tile([P, L * N], BF16, name="g_bf", align_bytes=64)
        for part, copy in zip(halves, (nc.vector.tensor_copy, nc.vector.tensor_copy)):
            weave(g_bf[:, L * part.start : L * part.stop], g_flat[:, :, part], copy)
        g_codes, g_scales = quantise("g", g_bf, E5M2, (256, 256))

        xm_bf = keep.tile([P, L * D], BF16, name="xm_bf", align_bytes=64)
        grad = {}
        deal(xm_bf, xm_raw, slice(0, 2), nc.scalar.copy)

        def gradient_pair(u, codes):
            xm_codes, xm_scales = quantise(f"xm{u}", xm_bf[:, 2 * u * D : 2 * (u + 1) * D], E4M3, (256,), codes)
            for j in (2 * u, 2 * u + 1):
                cols = slice((j % 2) * P, (j % 2 + 1) * P)
                for h, part in enumerate(halves if j == 0 else [whole]):
                    bank = psum.tile([P, N], F32, name=f"grad{j}_{h}", tag="score0" if j + h == 0 else f"grad{j}")
                    nc.tensor.matmul_mx(out=bank[:, part], lhsT=xm_codes[:, cols].bitcast(E4M3), lhsT_scale=xm_scales[:, cols], rhs=g_codes[:, part].bitcast(E5M2), rhs_scale=g_scales[:, part], start=True, stop=True)
                    grad[j, h] = bank
                grad[j, 1] = bank

        gradient_pair(0, None)
        deal(xm_bf, xm_raw, slice(2, 4), nc.vector.tensor_copy)
        gradient_pair(1, None)

        m_val = keep.tile([P, L, N], F32, name="m_val")
        steps = [keep.tile([P, N], F32, name=f"step{j}")[:] for j in range(L)]
        m_new = [keep.tile([P, T], F32, name=f"m_new{j}", tag=f"table{j}") for j in range(L)]
        loaded = slice(0, T // 2)
        copied = slice(T // 2, T)
        nc.sync.dma_start(m_new[2][:, loaded], m_planes[:, 2, loaded])
        nc.sync.dma_start(m_src[3][:], m_planes[:, 3, :])
        nc.sync.dma_start(m_new[3][:], m_planes[:, 3, :])

        def scatter_on_scalar(window, values, part):
            nc.scalar.activation(listed(window, part), values, COPY)

        def gather(j):
            nc.vector.tensor_scalar(steps[j], listed(m_src[j], whole), MOM_STEP, 0.0, MULT, ADD)

        def momentum(dst, j, part):
            nc.vector.scalar_tensor_tensor(dst, steps[j][:, part], BETA / MOM_STEP, grad[j, part.start // (N // 2)][:, part], MULT, ADD)

        def descend(dst, j, part, src):
            nc.vector.scalar_tensor_tensor(dst, grad[j, part.start // (N // 2)][:, part], GRAD_STEP, src, MULT, ADD)

        nc.scalar.activation(m_new[0][:, : T // 2], m_src[0][:, : T // 2], COPY)
        for part, scale in zip(halves, (LR * BETA / GRAD_STEP, MOM_STEP)):
            nc.scalar.activation(steps[0][:, part], listed(m_src[0], part), COPY, scale=scale)
        over_step = keep.tile([P, N // 2], F32, name="over_step")[:]
        nc.scalar.activation(over_step, w_got[:, 0, first], COPY, scale=1.0 / GRAD_STEP)
        nc.vector.tensor_copy(m_new[0][:, T // 2 :], m_src[0][:, T // 2 :])
        flat = shared.tile([P, L * T], BF16, name="rounded", offset=0, align_bytes=64)
        rounded = flat[:].rearrange("p (j t) -> p j t", j=L)
        early = flat[:, : 2 * N].bitcast(F32)
        spare = flat[:, 3 * T : 3 * T + 2 * N].bitcast(F32)
        late = flat[:, 2 * T - N : 2 * T + N].bitcast(F32)
        nc.vector.scalar_tensor_tensor(m_val[:, 0, first], steps[0][:, first], GRAD_STEP / LR, grad[0, 0][:, first], MULT, ADD)
        descend(late[:, second], 0, second, w_got[:, 0, second])
        nc.gpsimd.tensor_tensor(late[:, first], over_step, steps[0][:, first], ADD)
        nc.gpsimd.tensor_tensor(w_got[:, 0, first], late[:, first], m_val[:, 0, first], ADD)
        momentum(m_val[:, 0, second], 0, second)
        nc.gpsimd.tensor_tensor(steps[0][:, second], late[:, second], steps[0][:, second], ADD)
        descend(spare, 1, whole, w_got[:, 1, :])
        scatter_on_scalar(m_new[0], m_val[:, 0, first], first)
        nc.scalar.activation(listed(w_new[0], first), w_got[:, 0, first], COPY, scale=GRAD_STEP)
        scatter_on_scalar(m_new[0], m_val[:, 0, second], second)
        scatter_on_scalar(w_new[0], steps[0][:, second], second)
        descend(early, 2, whole, w_got[:, 2, :])
        gather(1)
        nc.vector.tensor_copy(m_new[1][:], m_src[1][:])
        new1 = keep.tile([P, N], F32, name="new1", tag="mom1", align_bytes=64)[:]
        nc.gpsimd.tensor_tensor(new1, spare, steps[1], ADD)
        momentum(m_val[:, 1, first], 1, first)
        scatter_on_scalar(m_new[1], m_val[:, 1, first], first)
        scatter_on_scalar(w_new[1], new1[:, first], first)
        gather(2)
        nc.vector.tensor_copy(m_new[2][:, copied], m_src[2][:, copied])
        nc.vector.tensor_tensor(late, early, steps[2], ADD)
        held = keep.tile([P, N // 2], F32, name="held", tag="mom2", align_bytes=64)[:]
        momentum(held, 1, second)
        scatter_on_scalar(w_new[1], new1[:, second], second)
        scatter_on_scalar(m_new[1], held, second)
        nc.vector.tensor_copy(listed(w_new[2], whole), late)
        momentum(m_val[:, 2, first], 2, first)
        descend(late, 3, whole, w_got[:, 3, :])
        scatter_on_scalar(m_new[2], m_val[:, 2, first], first)
        for part in halves:
            nc.vector.tensor_copy(steps[3][:, part], listed(m_src[3], part))
        for part in halves:
            nc.vector.scalar_tensor_tensor(w_got[:, 3, part], steps[3][:, part], MOM_STEP, late[:, part], MULT, ADD)
        kept = keep.tile([P, N // 2], F32, name="kept", tag="mom3", align_bytes=64)[:]
        momentum(kept, 2, second)
        nc.vector.tensor_copy(listed(w_new[3], whole), w_got[:, 3, :])
        nc.vector.scalar_tensor_tensor(w_got[:, 3, :], steps[3], BETA, grad[3, 0][:], MULT, ADD)
        nc.vector.tensor_copy(rounded[:, 3, quarter : 2 * quarter], w_new[3][:, quarter : 2 * quarter])
        nc.scalar.activation(rounded[:, 3, 2 * quarter :], w_new[3][:, 2 * quarter :], COPY)
        scatter_on_scalar(m_new[2], kept, second)
        for part in halves:
            scatter_on_scalar(m_new[3], w_got[:, 3, part], part)
        for planes, tables, j in ((o1_planes, m_new, 0), (o0_planes, w_new, 0), (o0_planes, w_new, 2), (o0_planes, w_new, 1), (o1_planes, m_new, 1), (o0_planes, w_new, 3), (o1_planes, m_new, 2)):
            nc.sync.dma_start(planes[:, j, :], tables[j][:])

        for j, start, stop in ((0, 0, 8), (2, 3, 8), (2, 0, 3), (1, 0, 8), (3, 0, 2)):
            part = slice(start * T // 8, stop * T // 8)
            nc.gpsimd.tensor_copy(rounded[:, j, part], w_new[j][:, part])
        out_scales = keep.tile([P, quarter], U8, name="out_scales", align_bytes=64)
        out_codes = [keep.tile([P, width], U32, name=f"out_codes{k}", align_bytes=64) for k, width in enumerate((quarter,) * 4)]
        for q in range(4):
            cols = slice(q * quarter, (q + 1) * quarter)
            out_bf = keep.tile([P, L * quarter], BF16, name=f"out_bf{q}", align_bytes=64)
            weave(out_bf[:], rounded[:, :, cols], nc.vector.tensor_copy)
            nc.vector.quantize_mx(out=out_codes[q][:].bitcast(E4M3), scales=out_scales[4 * q :, :], in_=out_bf[:])
            nc.sync.dma_start(words_out[:, cols], out_codes[q][:].bitcast(I32))
            if q == 1:
                nc.sync.dma_start(o1_planes[:, 3, :], m_new[3][:])
        for f in range(4):
            nc.sync.dma_start(scales_out[4 * f : 4 * f + 4, :].rearrange("i (q c) -> q i c", q=4), out_scales[32 * f : 32 * f + 16, :].bitcast(I32))
